import numpy as np, ml_dtypes
CORES = [2,3,42,43,82,83,122,123]
N = 8
BF = ml_dtypes.bfloat16
def gentries(a):
    return np.ascontiguousarray(a.reshape(8, 16, -1).transpose(0, 2, 1)).reshape(8, -1)
def gtable(e):
    e = np.asarray(e); return np.ascontiguousarray(e.reshape(8, -1, 16).transpose(0, 2, 1)).reshape(128, -1).astype(np.int32)
V, B, H, C, A, RO = 512, 96, 16, 32, 2, 2
def names(rng, hub, *shape):
    g = np.arange(8).reshape((1, 8) + (1,) * (len(shape) - 2))
    return np.where(rng.random(shape) < 0.15, hub[g, rng.integers(0, 8, shape)], rng.integers(0, N * V, shape))
def place(rng, d, nm):
    return np.where(np.argsort(rng.random((N, 8, 16, V)), axis=2) < d[:, :, None, :], nm, N * V)
def plain(rng):
    hub = rng.integers(0, N * V, (8, 8))
    few = rng.choice(np.array([0.5, 1.0, 2.0, 3.0]), (N, 8, 1)) * H
    d = np.where(rng.random((N, 8, V)) < 0.03, 0, rng.integers(1, 13, (N, 8, V)))
    d = np.where(rng.random((N, 8, V)) * V < few, rng.integers(13, 17, (N, 8, V)), d)
    tall = rng.random((N, 8, 1, V)) * V < 0.5 * H
    x = (40000 * (0.7 + 0.3 * rng.random((N, 8, 1, V))) * rng.random((N, 8, 16, V))).astype(np.int64)
    x = np.where(tall, rng.integers(40000, 65536, (N, 8, 16, V)), x)
    a = rng.integers(0, V, (N, 8, RO * B)); b = names(rng, hub, N, 8, RO * B)
    return x, d, names(rng, hub, N, 8, 16, V), a, b, rng.integers(-2000, 2001, (N, 128, RO))
def pack(x, L, a, b, u):
    return {"x0": np.ascontiguousarray(x.reshape(N, 128, V)).astype(np.int32), "l0": np.ascontiguousarray(L.reshape(N, 128, V)).astype(np.int32),
            "ea": np.stack([gtable(k) for k in a]), "eb": np.stack([gtable(k) for k in b]), "u": np.ascontiguousarray(u).astype(np.int32)}
def tops(x, L):
    tab = np.concatenate([x[q] for q in range(N)] + [np.zeros((8, 16, 1), np.int64)], axis=2)
    m = np.zeros_like(x)
    for q in range(N):
        for i in range(16): m[q] = np.maximum(m[q], np.take_along_axis(tab, L[q, :, i][:, None, :], 2))
    return m, tab
def setup_inputs(rng):
    x, d, nm, a, b, u = plain(rng)
    return pack(x, place(rng, d, nm), a, b, u)
def setup_inputs_room(rng):
    x, d, nm, a, b, u = plain(rng); L = place(rng, np.minimum(d, 12), nm)
    x[:, 7, :, ::2] |= 2 ** 15; x[:, 7, :, 1::2] >>= 3; a[:, 7, :B] -= a[:, 7, :B] % 2
    for g in range(8): x[:, g, rng.permutation(16)[:5]] = 0
    for q in range(N):
        b[q, :, :B] = q * V + rng.integers(0, V, (8, B))
        e = (q + 1) % N; b[q, 7, :B] = e * V + 1 + 2 * rng.permutation(V // 2)[:B]
        for g in range(8):
            m = H + (0, 1, H)[int(rng.integers(0, 3))]
            if g == 1: m = H
            vs = np.sort(rng.permutation(V)[:m])
            if g == 1: vs[H - 1] = V - 1
            n = rng.choice(np.array([0, 1, C - 1, C, C + 1]), N)
            if g == 0: n[:] = C
            if g == 7: n[e] = max(C - B, 0)
            n[q] = 0; n[q] = 16 * H - int(np.sum(n))
            own = rng.permutation(np.repeat(np.arange(N), n))
            L[q, g][:, vs[:H]] = (own * V + rng.integers(0, V, 16 * H)).reshape(H, 16).T
            L[q, g][:, vs[H:]] = rng.integers(0, N * V, (16, m - H))
    return pack(x, L, a, b, u)
def setup_inputs_ties(rng):
    x, d, nm, a, b, u = plain(rng); h = V // 2
    base = rng.integers(0, 50000, (8, 16)); base[rng.integers(0, 8)] = rng.integers(61500, 65001, 16)
    base = np.broadcast_to(base[None, :, :, None], (N, 8, 16, h))
    x[..., :h] = np.take_along_axis(base, np.argsort(rng.random((N, 8, 16, h)), axis=2), 2)
    x[:, :, 0, :h] += rng.integers(0, 2, (N, 8, h))
    nm = (nm // V) * V + nm % h; low = d[..., :h]
    d[..., :h] = np.where(low > 12, 13, np.where(rng.random((N, 8, h)) < 0.5, 12, low)); d[..., h:] = rng.integers(1, 13, (N, 8, h))
    L = place(rng, d, nm); top = tops(x, L)[0][..., h:]
    share = rng.choice(np.array([1.0, 2.0, 6.0]), (N, 8, 1, 1)) * H
    rows = np.where(rng.random((N, 8, 1, h)) * V < share, rng.integers(12, 14, (N, 8, 1, h)), 11)
    x[..., h:] = np.where(np.argsort(rng.random((N, 8, 16, h)), axis=2) < rows, top + 1, top)
    m = rng.random(a.shape) < 0.5
    a = np.where(m, a % h, a); b = np.where(m, (b // V) * V + b % h, b)
    own = a + (np.arange(N) * V)[:, None, None]; z = N // 2 * 2
    b = np.where(rng.random(a.shape) < 0.1, own, b)
    b[0:z:2, :, ::8] = own[1:z:2, :, ::8]; b[1:z:2, :, ::8] = own[0:z:2, :, ::8]
    return pack(x, L, a, b, rng.integers(-1, 2, u.shape))
def setup_inputs_crowd(rng):
    x, d, nm, a, b, u = plain(rng); q = np.arange(N) * V
    ends = np.concatenate([q, q + V - 1, q + V // 2])
    nm = np.where(rng.random(nm.shape) < 0.5, rng.choice(ends, nm.shape), nm); b = np.where(rng.random(b.shape) < 0.5, rng.choice(ends, b.shape), b)
    nm = np.where(rng.random((N, 8, 1, V)) < 0.2, nm[:, :, :1], nm)
    nm = np.where(rng.random(nm.shape) < 0.05, q[:, None, None, None] + np.arange(V), nm)
    d = rng.choice(np.array([16, 15, 14, 13, 12, 10, 4]), (N, 8, V))
    d = np.where(np.arange(V) < rng.integers(0, V // 2, (N, 8, 1)), np.minimum(d, 12), d)
    d[:, :, 0] = np.array([16, 15, 14, 13, 12, 11, 14, 15]); d[:, :, V - 1] = np.array([13, 14, 16, 15, 11, 12, 16, 13]); d[:, :, V // 2] = rng.integers(11, 17, (N, 8))
    L = place(rng, d, nm)
    for g in (6, 7):
        o = int(rng.integers(0, N)); v = int(rng.integers(C // 16, V))
        b[:, g, :B] = o * V + v; L[:, g, :, :C // 16] = o * V + v
        x[o, g, :, v] = 0; L[o, g, rng.permutation(16)[:8], v] = N * V
    return pack(x, L, a, b, u)
def setup_inputs_quiet(rng):
    x, d, nm, a, b, u = plain(rng); g = rng.permutation(8); q = rng.permutation(N)
    d[q[0], g[2:]] = 16; d[q[1], g[2:]] = np.minimum(d[q[1], g[2:]], 12)
    d[:, g[0]] = 0; d[:, g[1]] = np.minimum(d[:, g[1]], 12); x[:, g[1], rng.permutation(16)[:5]] = 0
    d[q[2], g[1], V - 1] = 16
    z = rng.random(u.shape)
    u = np.where(z < 0.125, rng.choice(np.array([-65535, 65535]), u.shape), np.where(z < 0.375, rng.integers(-65535, 65536, u.shape), u))
    k = int(g[0]); x[:, k] = np.array(x[0, k, :, :1]); u[:, 16 * k:16 * k + 16] = np.array(u[0, 16 * k:16 * k + 16])
    return pack(x, place(rng, d, nm), a, b, u)
def setup_inputs_spread(rng):
    x, d, nm, a, b, u = plain(rng)
    x = np.minimum((np.exp2(16 * rng.random((N, 8, 1, V))) * rng.random((N, 8, 16, V))).astype(np.int64), 65535)
    d = (17 * rng.random((N, 8, V)) * rng.random((N, 8, V))).astype(np.int64)
    nm = (N * V * rng.random(nm.shape) * rng.random(nm.shape)).astype(np.int64)
    a = (V * rng.random(a.shape) * rng.random(a.shape)).astype(np.int64); b = (N * V * rng.random(b.shape) * rng.random(b.shape)).astype(np.int64)
    u = np.exp2(14 * rng.random(u.shape)).astype(np.int64) * rng.choice(np.array([-1, 1]), u.shape)
    return pack(x, place(rng, d, nm), a, b, u)
def check_inputs(d):
    bad = []
    for k, lo, hi in (("x0", 0, 65535), ("l0", 0, N * V), ("ea", 0, V - 1), ("eb", 0, N * V - 1), ("u", -65535, 65535)):
        if np.min(d[k]) < lo or np.max(d[k]) > hi: bad.append("range of " + k)
    return bad
def reference(x0, l0, ea, eb, u):
    none = N * V
    x = x0.astype(np.int64).reshape(N, 8, 16, V); L = l0.astype(np.int64).reshape(N, 8, 16, V); dr = u.astype(np.int64).reshape(N, 8, 16, RO)
    a = np.stack([gentries(k) for k in ea]).astype(np.int64); b = np.stack([gentries(k) for k in eb]).astype(np.int64)
    for t in range(RO):
        M, tab = tops(x, L); tot = np.add.reduce(tab, axis=1)
        deg = np.add.reduce((L < none).astype(np.int64), axis=2); votes = np.add.reduce((x > M).astype(np.int64), axis=2)
        inv = (deg > 12) | ((deg > 0) & (votes >= 12))
        inv = inv & (np.add.accumulate(inv.astype(np.int64), axis=2) <= H)
        new = np.array(L)
        for g in range(8):
            come = [[] for d in range(N)]
            for q in range(N):
                aa = a[q, g, t * B:(t + 1) * B] + q * V; bb = b[q, g, t * B:(t + 1) * B]; first = tot[g, aa] <= tot[g, bb]
                vs = np.nonzero(inv[q, g])[0]
                rec = np.concatenate([np.where(first, aa, bb), L[q, g][:, vs].T.reshape(-1)])
                giv = np.concatenate([np.where(first, bb, aa), np.repeat(vs + q * V, 16)])
                row = np.concatenate([np.full(B, -1), np.tile(np.arange(16), len(vs))])
                for d in range(N):
                    for s in np.nonzero((rec >= d * V) & (rec < (d + 1) * V))[0][:C]: come[d].append((int(rec[s]) - d * V, int(giv[s]), q, int(row[s])))
            for d in range(N):
                seen = {}
                for v, w, q, i in come[d]:
                    k = seen.get(v, 0); seen[v] = k + 1
                    if k >= A: continue
                    empty = np.nonzero(L[d, g, :, v] == none)[0]
                    if k < len(empty):
                        new[d, g, empty[k], v] = w
                        if i >= 0: new[q, g, i, w - q * V] = none
        x = np.clip(((x + M) >> 1) + dr[..., t:t + 1], 0, 65535); L = new
    return {"yx": x.reshape(N, 128, V).astype(np.float32), "yl": L.reshape(N, 128, V).astype(np.float32)}

@@ -1,0 +1,583 @@
+from concourse.bass import DstId, RemoteDMATransfer
+from concourse.mybir import AluOpType as OP, ActivationFunctionType as AF, AxisListType
+
+N, V, B = 8, 512, 96
+NV = N * V
+K1 = 768
+SPARE = K1 + V
+WIN = SPARE + 256
+F32, BF, I32, U16 = "float32", "bfloat16", "int32", "uint16"
+MAGIC = 12582912.0
+
+
+def _sb(w, d):
+    return ("sbuf", [128, w], d)
+
+
+SCRATCH = {
+    "se": ("dram", [8, 128, 4], I32), "sx": ("dram", [8, 128, 64], U16), "sl": ("dram", [8, 128, 64], U16),
+    "le": ("dram", [8, 128, 4], I32), "lx": ("dram", [8, 128, 64], U16), "ll": ("dram", [8, 128, 64], U16),
+    "dx": ("dram", [8, 128, 64], F32), "rx": ("dram", [8, 128, 64], F32),
+    "dl": ("dram", [8, 128, 64], U16), "rl": ("dram", [8, 128, 64], U16),
+    "xi": _sb(512, I32), "li": _sb(512, I32), "es": _sb(32, I32), "eu": _sb(32, I32),
+    "xs": _sb(512, U16), "ls": _sb(512, U16), "xu": _sb(512, U16), "lu": _sb(512, U16),
+    "ou": _sb(512, U16), "of": _sb(512, F32),
+    "tt": _sb(NV + 16, F32), "gg": _sb(8192, F32), "ms": _sb(8192, F32), "lw": _sb(WIN, F32),
+    "hl": _sb(1024, BF), "a1": _sb(512, F32), "a2": _sb(512, F32), "xo": _sb(512, F32),
+    "rep": _sb(512, BF), "jr": _sb(512, BF), "one": _sb(512, BF), "seg": _sb(1536, BF), "j16": _sb(256, BF), "diag": _sb(256, BF),
+    "iv": _sb(512, F32), "pi": _sb(4, I32), "pt": _sb(8, I32), "cc": _sb(32, F32),
+    "tb": _sb(NV + 16, BF), "tb2": _sb(NV, BF), "iom": _sb(NV, F32), "base": _sb(512, BF), "base2": _sb(512, BF),
+    "c2": _sb(8, F32), "nrow": _sb(528, F32), "bits": _sb(528, BF), "bito": _sb(528, BF),
+    "bi": _sb(512, I32), "bj": _sb(512, I32), "bk": _sb(512, I32),
+    "jg": _sb(128, BF), "bo": _sb(128, BF), "bof": _sb(128, F32), "bo9": _sb(128, BF), "idb": _sb(128, BF), "idf": _sb(128, F32),
+    "nid": _sb(128, BF), "it": _sb(128, BF), "nit": _sb(128, BF), "tri": _sb(128, BF), "lt": _sb(128, BF),
+    "jlo": _sb(128, BF), "jhi": _sb(128, BF),
+    "gq": _sb(8, F32), "rw": _sb(16, BF), "kr": _sb(128, BF), "kt": _sb(128, BF), "thr": _sb(128, BF), "dth": _sb(96, F32),
+    "db": _sb(64, F32), "exi": _sb(16, I32), "exu": _sb(16, U16), "k1": _sb(2, BF), "pw": _sb(64, F32),
+    "emp": _sb(512, BF), "s1": _sb(512, BF), "s2": _sb(512, BF), "et": _sb(WIN, BF), "ne": _sb(528, BF),
+    "gt": _sb(512, BF), "sg": _sb(512, BF), "cum": _sb(512, BF), "junk": _sb(512, BF), "sm": _sb(16, F32),
+    "us": _sb(128, U16), "ue": _sb(24, U16), "ed": _sb(96, F32), "edi": _sb(32, I32), "gb": _sb(96, F32), "df": _sb(96, F32),
+    "p1": _sb(352, BF), "p2": _sb(352, BF), "cn": _sb(352, BF), "pr": _sb(352, BF), "ym": _sb(352, BF), "ys": _sb(352, BF),
+    "zz": _sb(176, F32), "ww": _sb(608, BF), "zb": _sb(256, BF), "zo": _sb(256, BF), "gbr": _sb(256, F32),
+    "nm": _sb(256, BF), "ns": _sb(256, BF), "dlt": _sb(256, F32), "val": _sb(256, F32), "ax": _sb(256, BF), "aw": _sb(512, BF),
+    "am": _sb(256, BF), "ak": _sb(256, BF),
+    "e00": ("sbuf", [128, 8, 128], BF), "e01": ("sbuf", [128, 8, 128], BF), "e11": ("sbuf", [128, 8, 128], BF),
+}
+for _k in range(8):
+    SCRATCH["p%d_" % _k] = ("psum", [128, 512], F32)
+NDMA = 24
+SEMAPHORES = ["sv", "sa", "sp", "sg", "ae", "ax", "al", "bx", "bl", "out"] + ["d%d" % k for k in range(NDMA)]
+
+
+def program(rank, T, topo):
+    ops = []
+
+    def A(name, c0=0, c1=None, step=1, p0=0, p1=128):
+        if c1 is None:
+            c1 = SCRATCH[name][1][1]
+        return ("ap", name, c0, c1, step, p0, p1)
+
+    def col(name, c):
+        return A(name, c, c + 1)
+
+    def P(k, c0=0, c1=512, step=1, p0=0, p1=128):
+        return A("p%d_" % k, c0, c1, step, p0, p1)
+
+    def IND(win, off):
+        return ("ind", win, off)
+
+    def RAW(name, ap, c0=0, c1=1 << 20):
+        return ("raw", name, ap, c0, c1)
+
+    def put(q, call, args, kw=None, nout=1, extra_out=()):
+        ops.append((q, call, args, kw or {}, nout, extra_out))
+
+    def tc(out, in_): put("v", "tensor_copy", [out, in_])
+    def tt(out, a, b, op): put("v", "tensor_tensor", [out, a, b, op])
+    def ts(out, a, s1, op0, s2=None, op1=None):
+        put("v", "tensor_scalar", [out, a, s1, s2, op0] + ([op1] if op1 is not None else []))
+    def scan(out, d0, d1, init, op0, op1): put("v", "tensor_tensor_scan", [out, d0, d1, init, op0, op1])
+    def ms(out, c): put("v", "memset", [out, c])
+    def act(out, in_, f, bias=None, scale=None, acc=None):
+        kw = {}
+        if bias is not None: kw["bias"] = bias
+        if scale is not None: kw["scale"] = scale
+        if acc is not None: kw["accum_out"] = acc
+        put("a", "activation", [out, in_, f], kw, 1, (acc,) if acc is not None else ())
+    def mm(out, l, r, st=True, sp=True): put("p", "matmul", [out, l, r, st, sp])
+    def iota(out, pat, base=0, cm=0):
+        put("g", "iota", [out, pat, base, cm], {} if SCRATCH[out[1]][2] == I32 else {"allow_small_or_imprecise_dtypes": True})
+    def dma(q, out, in_): put(q, "dma_start", [out, in_])
+
+    me = T.cores[rank]
+    own = dict(p0=16 * rank, p1=16 * rank + 16)
+
+    def exchange(buf, src, dst, sem, q2="s"):
+        dma("s", RAW(src, T[src][:]), A(buf))
+        dma(q2, RAW(dst, T[dst][rank]), A(buf, **own))
+        far = [r for r in range(N) if r != rank and topo.chip(T.cores[r]) != topo.chip(me)]
+        used, tr, total = set(), [], 0
+        for r in far + [r for r in range(N) if r != rank and r not in far]:
+            free = [e for e in topo.engines(me, T.cores[r]) if e not in used]
+            take = free[:1] if r in far else free[-1:]
+            used.update(take)
+            rid, pid, _ = topo.addr(T.cores[r])
+            tr.append(RemoteDMATransfer(dst_ids=[DstId(rid=rid, pnc=pid)], dma_engine_mask=sum(1 << e for e in take),
+                                        remote_sem=T.sem[sem], src=T[src][r], dst=T[dst][rank]))
+            total += len(take)
+        ops.append(("g", "remote", [RAW(src, None), tr, total], {}, 0, ()))
+
+    def landed(dst, sem):
+        ops.append(("x", "landed", [RAW(dst, None), sem, N - 1], {}, 1, ()))
+
+    C = {k: col("cc", i) for i, k in enumerate(
+        ["pm", "pg", "od", "p32", "p64", "pf", "g512", "b2", "b3", "key", "cb", "ic", "le8", "pw", "x1", "x2", "x3", "x4",
+         "m1", "m2", "m3", "p64h"])}
+    D = lambda k: col("diag", k)
+
+    ms(A("es", 24, 32), 0)
+    dma("s", A("xi"), RAW("x0", T.x0[:]))
+    dma("a", A("es", 0, 12), RAW("ea", T.ea[:]))
+    dma("s", A("es", 12, 24), RAW("eb", T.eb[:]))
+    dma("a", A("es", 24, 26), RAW("u", T.u[:]))
+    dma("a", A("li"), RAW("l0", T.l0[:]))
+    iota(col("pi", 0), [[0, 1]], 0, 1)
+    iota(A("j16"), [[0, 16], [1, 16]])
+    iota(A("iv"), [[1, 512]])
+    exchange("es", "se", "le", "ae", "a")
+    ms(A("pw", 0, 16), 0.5)
+    ms(A("pw", 16, 32), 0.0)
+    ts(col("pt", 0), col("pi", 0), 15, OP.bitwise_and)
+    ts(col("pt", 1), col("pi", 0), 4, OP.arith_shift_right)
+    ts(col("pt", 2), col("pi", 0), 4, OP.arith_shift_right, 1, OP.bitwise_and)
+    ts(col("pt", 3), col("pi", 0), 96, OP.bitwise_and)
+    ts(col("pt", 4), col("pi", 0), 63, OP.bitwise_and)
+    scan(A("pw", 32, 48), A("pw", 0, 16), A("pw", 16, 32), 2.0, OP.mult, OP.add)
+    tc(C["pf"], col("pi", 0))
+    tc(A("cc", 0, 5), A("pt", 0, 5))
+    ms(A("pw", 41, 45), 1.0)
+    ms(A("one"), 1.0)
+    ms(A("pw", 41, 45, 2), 1.0 / 64)
+    ts(A("diag"), A("j16"), C["pm"], OP.is_equal)
+    ts(C["g512"], C["pg"], 512.0, OP.mult)
+    tt(A("pw", 48, 64), A("pw", 32, 48), A("diag", 0, 16), OP.mult)
+    ts(C["m1"], D(9), D(10), OP.add)
+    ts(C["m2"], D(9), -64.0, OP.mult)
+    put("v", "tensor_reduce", [C["pw"], A("pw", 48, 64), AxisListType.X, OP.add])
+    ts(C["m3"], D(11), D(12), OP.add)
+    ts(A("c2"), A("j16", 0, 8), 8.0, OP.mult, D(11), OP.mult)
+    act(A("a1"), A("iv"), AF.Identity, bias=-0.499, scale=C["pw"])
+    tc(A("xs"), A("xi"))
+    exchange("xs", "sx", "lx", "ax")
+    tc(A("ls"), A("li"))
+    exchange("ls", "sl", "ll", "al")
+    iota(A("jr"), [[16, 4], [0, 8], [1, 16]])
+    iota(A("jg"), [[1, 8], [0, 16]])
+    iota(A("kr"), [[32, 4], [1, 2], [2, 16]])
+    iota(A("exi"), [[1, 2], [2, 8]])
+    iota(A("ww"), [[0, 608]])
+    iota(A("lw", 512, 528), [[0, 16]], NV)
+    iota(A("lw", 528, WIN), [[0, WIN - 528]])
+    iota(A("et"), [[0, WIN]])
+    iota(A("aw"), [[0, 512]])
+    iota(A("iom"), [[1, NV]], -NV)
+
+    tc(A("bi"), A("a1"))
+    ms(A("seg"), 1.0)
+    ts(A("bk"), A("bi"), 63, OP.bitwise_and)
+    ts(A("bj"), A("bi"), 1, OP.bitwise_and)
+    ts(A("base"), A("bk"), C["m1"], OP.mult, C["m2"], OP.add)
+    ts(A("base2"), A("bk"), C["m3"], OP.mult)
+    for q in range(N):
+        act(A("tb", q * V, q * V + V), A("base"), AF.Identity, bias=D(q))
+    for q in range(N):
+        act(A("tb2", q * V, q * V + V), A("base2"), AF.Identity, bias=col("c2", q))
+    ms(A("seg", 0, 1536, 16), 0.0)
+    ms(A("k1"), float(K1))
+    ms(A("tt", NV, NV + 16), 0.0)
+    ms(A("ne", 512, 528), 2.0 * K1)
+    ms(A("nrow", 512, 528), 0.0)
+    ms(A("bits", 512, 528), 0.0)
+    ms(A("bito", 512, 528), 0.0)
+    ts(C["x1"], D(9), 64.0, OP.mult, D(10), OP.add)
+    ts(C["x2"], D(11), 64.0, OP.mult, D(12), OP.add)
+    ts(C["b2"], C["pm"], 9.0, OP.is_lt, 2.0, OP.mult)
+    ts(C["b3"], C["pm"], 9.0, OP.is_lt, -1.0, OP.mult)
+    ts(C["cb"], C["pm"], 2.0, OP.mult, 1.0, OP.add)
+    ts(C["x3"], C["pm"], 8.0, OP.is_ge, 33.0, OP.mult)
+    ts(C["le8"], C["pm"], 8.0, OP.is_le)
+    ts(C["x4"], C["pm"], 2.0, OP.mult, C["od"], OP.add)
+    ts(C["p64h"], C["p64"], 64.0, OP.add)
+    ts(A("gq"), A("j16", 0, 8), C["pg"], OP.is_equal)
+    ts(A("db", 0, 16), A("j16", 0, 16), 16.0, OP.mult, C["pm"], OP.add)
+    ts(A("dth"), A("diag", 0, 96), -1.0, OP.add, 1.0e7, OP.mult)
+    ts(C["ic"], C["x3"], -32.0, OP.add)
+    ts(C["key"], C["x4"], C["p32"], OP.add)
+    ts(A("rw", 0, 8), A("gq"), C["x1"], OP.mult)
+    ts(A("rw", 8, 16), A("gq"), C["x2"], OP.mult)
+    ts(A("db", 16, 32), A("db", 0, 16), 256.0 - 31, OP.add)
+    ts(A("db", 32, 48), A("db", 0, 16), 512.0 - 31, OP.add)
+    ts(A("db", 48, 64), A("db", 0, 16), float(SPARE - NV), OP.add)
+    ts(A("tb", NV, NV + 16), A("one", 0, 16), D(8), OP.mult)
+    ts(A("idb"), A("iv", 0, 128), C["pf"], OP.is_equal)
+    ts(A("nid"), A("iv", 0, 128), C["pf"], OP.is_equal, -1.0, OP.mult)
+    ts(A("lt"), A("iv", 0, 128), C["pf"], OP.is_gt)
+    ts(A("idf"), A("iv", 0, 128), C["pf"], OP.is_equal)
+    ts(A("jlo"), A("iv", 0, 128), C["p64"], OP.is_equal)
+    ts(A("jhi"), A("iv", 0, 128), C["p64h"], OP.is_equal)
+    ts(A("bits", 0, 512), A("bj"), C["b2"], OP.mult, C["b3"], OP.add)
+    ts(A("nrow", 0, 512), A("iv"), C["g512"], OP.add)
+    ts(A("bito", 0, 512), A("bits", 0, 512), C["od"], OP.mult)
+    ts(A("rep"), A("jr"), C["p64"], OP.is_equal)
+    ts(A("bo"), A("jg"), C["pg"], OP.is_equal)
+    ts(A("bof"), A("jg"), C["pg"], OP.is_equal)
+    ts(A("bo9"), A("jg"), C["pg"], OP.is_equal, C["le8"], OP.mult)
+    tt(A("tri"), A("lt"), A("bo"), OP.mult)
+    ts(A("kt"), A("kr"), C["key"], OP.is_le, 90.0, OP.mult)
+    tc(A("exu"), A("exi"))
+    tt(A("it"), A("idb"), A("tri"), OP.subtract)
+    tt(A("nit"), A("tri"), A("idb"), OP.subtract)
+    ts(A("thr"), A("kt"), 9.0, OP.add)
+
+    landed("le", "ae")
+    dma("s", A("eu"), RAW("le", T.le[:]))
+    landed("lx", "ax")
+    dma("s", A("xu"), RAW("lx", T.lx[:]))
+    landed("ll", "al")
+    dma("s", A("lu"), RAW("ll", T.ll[:]))
+    ts(A("ed", 0, 12), A("eu", 0, 12), C["g512"], OP.add)
+    tc(A("ed", 12, 24), A("eu", 12, 24))
+    ts(A("sm", 8, 10), A("eu", 24, 26), -0.25, OP.add)
+    tc(A("ue"), A("ed", 0, 24))
+    tt(A("ed", 24, 36), A("ed", 0, 12), A("ed", 12, 24), OP.subtract)
+
+    HL = lambda h, up: A("hl", 512 * h, 512 * h + 512, 1, 64 * up, 64 * up + 64)
+
+    def low(h):
+        tt(HL(h, 1 - h), P(0, p0=64 * h, p1=64 * h + 64), HL(h, h), OP.subtract)
+
+    def table(q, bank, eng):
+        mm(P(bank), A("rep", 128 * (q % 4), 128 * (q % 4) + 128), A("hl", 512 * (q // 4), 512 * (q // 4) + 512))
+        if eng == "a":
+            act(A("tt", q * V, q * V + V), P(bank), AF.Copy)
+        else:
+            tc(A("tt", q * V, q * V + V), P(bank))
+
+    tc(P(0), A("xu"))
+    for h in range(2):
+        ts(HL(h, h), A("xu", p0=64 * h, p1=64 * h + 64), 1.0, OP.mult)
+        low(h)
+    for q in range(8):
+        table(q, 2 + q % 6, "v" if q in (3, 5, 7) else "a")
+
+    TW, TBW = A("tt"), A("tb")
+
+    def place(j0, n, rec, giv, own32, init, dump, pos, between=lambda: None):
+        k = n // 16
+        r = lambda name: A(name, j0, j0 + n)
+        tc(r("p1"), IND(TBW, rec))
+        act(r("p2"), IND(A("tb2"), giv), AF.Copy)
+        scan(r("cn"), r("p1"), A("one", 0, n), init, OP.add, OP.min)
+        tt(r("pr"), r("cn"), r("p1"), OP.mult)
+        mm(P(1, 0, n), A("bo9"), r("pr"))
+        between()
+        tt(r("ym"), P(1, 0, n), A("diag", 0, n), OP.mult)
+        scan(r("ys"), A("seg", 0, n), r("ym"), 0.0, OP.mult, OP.add)
+        y = A("ys", j0 + 15, j0 + n, 16)
+        tt(A("zz", 0, k), y, dump, OP.mult)
+        tt(A("zz", 16, 16 + k), y, own32, OP.add)
+        tt(A("zz", 32, 32 + k), A("zz", 0, k), A("zz", 16, 16 + k), OP.max)
+        ts(pos, A("zz", 32, 32 + k), 31.0, OP.add)
+        tt(IND(A("ww"), pos), r("p1"), r("p2"), OP.add)
+
+    def edges(t):
+        c = 6 * t
+        tc(A("gb"), IND(TW, A("ue", 12 + c, 18 + c)))
+        tt(A("df"), IND(TW, A("ue", c, c + 6)), A("gb"), OP.subtract)
+        mm(P(1, 0, B), A("bof"), A("df"))
+        yield
+        tt(A("ym", 256, 352), P(1, 0, B), A("dth"), OP.is_le)
+        scan(A("ys", 256, 352), A("seg", 0, B), A("ym", 256, 352), 0.0, OP.mult, OP.add)
+        tt(A("ed", 48, 54), A("ys", 256 + 15, 352, 16), A("ed", 24 + c, 30 + c), OP.mult)
+        tt(A("edi", 0, 6), A("ed", 48, 54), A("ed", 12 + c, 18 + c), OP.add)
+        tt(A("ed", 64, 70), A("ed", c, 6 + c), A("ed", 48, 54), OP.subtract)
+        tc(A("us", 12, 18), A("edi", 0, 6))
+        tc(A("us", 18, 24), A("ed", 64, 70))
+        ts(A("edi", 8, 14), A("edi", 0, 6), 4, OP.arith_shift_right, 0xE0, OP.bitwise_and)
+        yield
+        place(256, B, A("us", 12, 18), A("us", 18, 24), A("edi", 8, 14), C["ic"], A("db", 32, 38), A("us", 24, 30))
+
+    def gather(eng, v0, v1):
+        o, i = A("gg", 16 * v0, 16 * v1), IND(TW, A("lu", v0, v1))
+        if eng == "a":
+            act(o, i, AF.Copy)
+        else:
+            tc(o, i)
+
+    def top(v0, v1):
+        scan(A("ms", 16 * v0, 16 * v1), A("seg", 0, 16 * (v1 - v0)), A("gg", 16 * v0, 16 * v1), 0.0, OP.mult, OP.max)
+
+    def M(v0, v1):
+        return A("ms", 16 * v0 + 15, 16 * v1, 16)
+
+    def ripe(v0, v1, part):
+        if part == 0:
+            tt(A("gt", v0, v1), P(0, v0, v1), M(v0, v1), OP.is_gt)
+            mm(P(2, v0, v1), A("idb"), A("s1", v0, v1), True, False)
+            mm(P(2, v0, v1), A("nid"), A("s2", v0, v1), False, False)
+            mm(P(2, v0, v1), A("bo"), A("gt", v0, v1), False, True)
+            mm(P(4, v0, v1), A("jlo"), A("hl", v0, v1), True, False)
+            mm(P(4, v0, v1), A("jhi"), A("hl", 512 + v0, 512 + v1), False, False)
+            mm(P(4, v0, v1), A("idf"), M(v0, v1), False, True)
+        elif part == 1:
+            act(A("sg", v0, v1), P(2, v0, v1), AF.Sign, bias=-11.5)
+        elif part == 2:
+            scan(A("cum", v0, v1), A("sg", v0, v1), A("one", 0, v1 - v0), 0.0 if v0 == 0 else col("cum", v0 - 1), OP.add, OP.add)
+        else:
+            act(A("junk", v0, v1), A("cum", v0, v1), AF.Sign, bias=C["cb"], scale=-1.0, acc=col("sm", 0 if v0 == 0 else 4))
+
+    cuts = [[0, 48, 128, 224, 320, 400, 456, 492, 512], [0, 32, 112, 208, 304, 384, 448, 488, 512]]
+    for t in range(2):
+        last = t == 1
+        cut = cuts[t]
+        RA = cut[5]
+        e = edges(t)
+        gather("a", cut[1], cut[2])
+        next(e)
+        if t == 0:
+            tc(A("lw", 0, 512), A("lu"))
+        ts(A("emp"), A("lu"), float(NV), OP.is_equal)
+        mm(P(3), A("bo"), A("emp"))
+        next(e)
+        gather("a", cut[2], cut[3])
+        gather("v", cut[0], cut[1])
+        top(cut[0], cut[1])
+        top(cut[1], cut[2])
+        act(A("s1"), P(3), AF.Relu, bias=48.0, scale=-12.0)
+        act(A("s2"), P(3), AF.Relu, bias=-255.0, scale=17.0)
+        next(e, None)
+        mm(P(5), A("bo"), A("emp"))
+        mm(P(3), A("it"), A("emp"))
+        gather("a", cut[3], cut[4])
+        top(cut[2], cut[3])
+        gather("a", cut[4], cut[5])
+        top(cut[3], cut[4])
+        gather("a", cut[5], cut[6])
+        top(cut[4], cut[5])
+        ripe(0, RA, 0)
+        gather("a", cut[6], cut[7])
+        top(cut[5], cut[6])
+        gather("a", cut[7], cut[8])
+        ripe(0, RA, 1)
+        top(cut[6], cut[7])
+        ripe(0, RA, 2)
+        ripe(0, RA, 3)
+        top(cut[7], cut[8])
+        ripe(RA, 512, 0)
+        ts(col("sm", 1), col("sm", 0), 0.5, OP.mult, 256.0, OP.add)
+        act(A("et", 0, 512), P(3), AF.Relu)
+        for k in (1, 2, 3):
+            ripe(RA, 512, k)
+        vs, vsu = A("us", 32, 33), A("us", 34, 35)
+        ts(vs, col("sm", 4), 0.5, OP.mult, col("sm", 1), OP.add)
+        act(A("a1"), P(4), AF.Relu, bias=col("sm", 8 + t), scale=0.5)
+        mm(P(3), A("it"), A("emp"), True, False)
+        mm(P(3), A("nit"), A("et", 0, 512), False, True)
+        LWv = A("lw", 0, 528)
+        ri, gi, pos = A("us", 48, 64), A("us", 64, 80), A("us", 80, 96)
+        tc(ri, IND(LWv, vs))
+        tc(gi, IND(A("nrow"), vs))
+
+        def between():
+            tc(A("edi", 16, 32), ri)
+            ts(col("sm", 2), col("sm", 4), 0.5, OP.mult, col("sm", 1), OP.add)
+            ts(A("edi", 16, 32), A("edi", 16, 32), 4, OP.arith_shift_right, 0xE0, OP.bitwise_and)
+            act(A("a2"), A("a1"), AF.Identity, bias=MAGIC + 65535.0, scale=-1.0)
+            act(A("a1"), A("a2"), AF.Relu, bias=-MAGIC)
+            if last:
+                act(A("xo"), A("a1"), AF.Identity, bias=65535.0, scale=-1.0)
+                exchange("xo", "dx", "rx", "bx")
+            else:
+                act(P(0), A("a1"), AF.Identity, bias=65535.0, scale=-1.0)
+                for h in range(2):
+                    act(HL(h, h), A("a1", p0=64 * h, p1=64 * h + 64), AF.Identity, bias=65535.0, scale=-1.0)
+            act(A("ne", 0, 512), P(5), AF.Relu, bias=2.0 * K1, scale=-float(K1))
+            act(A("et", K1, K1 + V), P(3), AF.Relu)
+
+        place(0, 256, ri, gi, A("edi", 16, 32), col("cn", 351), A("db", 16, 32), pos, between)
+        for s in range(2):
+            mm(P(1, s, 32, 2), A("ww", s, 256, 2), A("rw"))
+        vo, go, off = A("us", 96, 112), A("us", 112, 128), A("us", 64, 80)
+        ts(vo, P(1, 0, 16), float(NV), OP.add, 512.0, OP.min)
+        tc(go, P(1, 16, 32))
+        tc(A("zb"), IND(A("bits"), vo))
+        act(A("zo"), IND(A("bito"), vo), AF.Copy)
+        tc(A("zz", 48, 64), P(1, 0, 16))
+        if not last:
+            low(0)
+        units = [("e00", 0, 0, dd, 2 + dd, 0) for dd in range(4)] + [("e01", 0, 1, dd, 6 + dd, 0) for dd in range(2)]
+        units += [("e11", 1, 1, dd, 2 + dd, 256) for dd in range(2)] + [("e01", 0, 1, dd, 4 + dd, 256) for dd in range(2, 4)]
+        units += [("e11", 1, 1, dd, 2 + dd, 256) for dd in range(2, 4)]
+        for nm, hr, hc, dd, bank, c0 in units:
+            for par in range(2):
+                p0 = 32 * dd
+                p1 = p0 + (32 if par else 16)
+                mm(P(bank, c0 + 128 * par, c0 + 128 * par + 128), A("zo" if par else "zb", 128 * hr, 128 * hr + 128, 1, p0, p1),
+                   A("zb", 128 * hc, 128 * hc + 128, 1, p0, p1))
+            for par in range(2):
+                d = 2 * dd + par
+                o = RAW(nm, T[nm][:, :, 16 * d:16 * d + 16], d, d + 1)
+                if hr == hc:
+                    tt(o, P(bank, c0 + 128 * par, c0 + 128 * par + 128), A("thr"), OP.is_ge)
+                else:
+                    act(o, P(bank, c0 + 128 * par, c0 + 128 * par + 128), AF.Relu, bias=-8.0)
+            if (nm, dd) == ("e00", 0):
+                act(A("gbr"), IND(A("iom"), go), AF.Copy)
+        for c in range(8):
+            mm(P(1, 64 + c, 65 + c), RAW("e00", T.e00[:, c, :]), col("k1", 0))
+        for c in range(8):
+            mm(P(1, 72 + c, 73 + c), RAW("e01", T.e01[:, c, :]), col("k1", 0), True, False)
+            mm(P(1, 72 + c, 73 + c), RAW("e11", T.e11[:, c, :]), col("k1", 0), False, True)
+        tt(A("nm"), IND(A("ne"), vo), A("diag"), OP.mult)
+        ts(col("sm", 3), col("sm", 2), 512.0, OP.is_ge, C["pm"], OP.mult)
+        scan(A("ns"), A("seg", 0, 256), A("nm"), 0.0, OP.mult, OP.add)
+        ts(vsu, col("sm", 3), col("sm", 2), OP.add)
+        ts(A("zz", 160, 176), A("ns", 15, 256, 16), -1.0, OP.mult, 2.0 * K1, OP.add)
+        kk = P(1, 64, 80)
+        tt(A("zz", 96, 112), kk, A("zz", 48, 64), OP.add)
+        tt(A("zz", 80, 96), kk, A("zz", 160, 176), OP.is_lt)
+        tt(A("zz", 112, 128), A("zz", 96, 112), A("db", 48, 64), OP.min)
+        act(A("ax"), IND(A("zz", 80, 96), A("exu")), AF.Copy)
+        ts(A("zz", 64, 80), ri, -1.0, OP.mult, float(NV), OP.add)
+        ts(off, A("zz", 112, 128), float(NV), OP.add)
+        if not last:
+            table(0, 6, "a")
+            low(1)
+        for s in range(2):
+            mm(P(2, s, 256, 2), A("ax", 128 * s, 128 * s + 128), A("idb"))
+        act(A("aw", 0, 256), P(2, 0, 256), AF.Copy)
+        if not last:
+            for q in range(1, 5):
+                table(q, 4 + (q + 2) % 4, "a")
+        tt(A("dlt"), IND(A("et"), off), A("gbr"), OP.mult)
+        tt(A("val"), IND(A("lw"), off), A("dlt"), OP.add)
+        tc(IND(A("lw"), off), A("val"))
+        act(P(3), A("lw", K1, K1 + V), AF.Copy)
+        if not last:
+            for q in range(5, 7):
+                table(q, 4 + (q + 2) % 4, "a")
+        tt(A("am"), IND(A("aw"), pos), A("diag"), OP.mult)
+        scan(A("ak"), A("seg", 0, 256), A("am"), 0.0, OP.mult, OP.add)
+        tt(A("zz", 128, 144), A("ak", 15, 256, 16), A("zz", 64, 80), OP.mult)
+        tt(A("zz", 144, 160), IND(LWv, vsu), A("zz", 128, 144), OP.add)
+        tc(IND(LWv, vsu), A("zz", 144, 160))
+        for v0, v1 in ([(0, 512)] if last else [(0, cuts[1][2]), (cuts[1][2], 512)]):
+            tt(A("lw", v0, v1), A("lw", v0, v1), P(3, v0, v1), OP.add)
+            tc(A("lu", v0, v1), A("lw", v0, v1))
+            if v1 < 512:
+                table(7, 5, "v")
+        if not last:
+            iota(A("lw", K1, K1 + V), [[0, V]])
+            iota(A("ww", 0, 256), [[0, 256]])
+
+    exchange("lu", "dl", "rl", "bl", "a")
+    landed("rx", "bx")
+    dma("a", RAW("yx", T.yx[:]), RAW("rx", T.rx[:]))
+    landed("rl", "bl")
+    dma("s", A("ou"), RAW("rl", T.rl[:]))
+    tc(A("of"), A("ou"))
+    dma("s", RAW("yl", T.yl[:]), A("of"))
+    return ops
+
+
+def spans(x):
+    if not isinstance(x, tuple) or not x or x[0] not in ("ap", "ind", "raw"):
+        return []
+    if x[0] == "ind":
+        return spans(x[1]) + spans(x[2])
+    if x[0] == "raw":
+        return [(x[1], x[3], x[4])]
+    if x[1].endswith("_"):
+        return [(x[1], 0, 1 << 20)]
+    return [(x[1], x[2], x[3])]
+
+
+def rank_program(g, core, T, topo):
+    rank = T.rank_of(core)
+    if rank is None:
+        return
+    ops = program(rank, T, topo)
+    queue = {"v": g.vector, "a": g.scalar, "p": g.tensor, "g": g, "s": g.sync}
+
+    def real(x):
+        if not isinstance(x, tuple) or not x or x[0] not in ("ap", "ind", "raw"):
+            return x
+        if x[0] == "raw":
+            return x[2]
+        if x[0] == "ind":
+            return real(x[1]).indirect(real(x[2]))
+        _, name, c0, c1, step, p0, p1 = x
+        return T[name][p0:p1, c0:c1:step] if step != 1 else T[name][p0:p1, c0:c1]
+
+    touch, deps = [], []
+    for q, call, args, kw, nout, extra in ops:
+        wr, rd = [], []
+        for x in list(args[:nout]) + list(extra):
+            if x[0] == "ind":
+                wr += spans(x[1]); rd += spans(x[2])
+            else:
+                wr += spans(x)
+        for x in list(args[nout:]) + [v for k, v in kw.items() if k != "accum_out"]:
+            rd += spans(x)
+        dma = call in ("dma_start", "remote", "landed")
+        mine = []
+        for j, (q2, wr2, rd2, dma2) in enumerate(touch):
+            if q == q2 == "p":
+                continue
+            hit = False
+            for n, a, b in wr:
+                for n2, a2, b2 in wr2 + rd2:
+                    if n == n2 and a < b2 and a2 < b and not (dma and dma2 and (n2, a2, b2) not in rd2):
+                        if not (n.endswith("_") and q == q2 and (n2, a2, b2) not in wr2):
+                            hit = True
+            for n, a, b in rd:
+                for n2, a2, b2 in wr2 + ([s for s in rd2 if s[0].endswith("_")] if q != q2 else []):
+                    if n == n2 and a < b2 and a2 < b:
+                        hit = True
+            if hit and call != "landed":
+                mine.append(j)
+        touch.append((q, wr, rd, dma))
+        deps.append(mine)
+    need = []
+    for i, mine in enumerate(deps):
+        latest = {}
+        keep = []
+        for j in mine:
+            if touch[j][3]:
+                keep.append(j)
+            else:
+                latest[touch[j][0]] = j
+        need.append(keep + list(latest.values()))
+    wanted = set(j for m in need for j in m)
+    mark, count, known, ndma, out = {}, {}, {k: {} for k in queue}, [0], [0]
+    for i, (q, call, args, kw, nout, extra) in enumerate(ops):
+        if call == "landed":
+            mark[i] = (args[1], args[2])
+            count[args[1]] = args[2]
+            continue
+        waits = {}
+        for j in need[i]:
+            if j in mark:
+                s, n = mark[j]
+                waits[s] = max(waits.get(s, 0), n)
+        for s, n in waits.items():
+            if known[q].get(s, 0) < n:
+                queue[q].wait_ge(T.sem[s], n)
+                known[q][s] = n
+        if call == "remote":
+            g.remote_dma_fused(args[1], local_sem=T.sem.out)
+            out[0] += args[2]
+            continue
+        a, k = [real(x) for x in args], {n: real(x) for n, x in kw.items()}
+        e = queue[q]
+        if call == "dma_start":
+            s = "d%d" % ndma[0]
+            ndma[0] += 1
+            e.dma_start(*a).then_inc(T.sem[s], 16)
+            mark[i] = (s, 16)
+            count[s] = 16
+            continue
+        ins = {"tensor_copy": lambda: e.tensor_copy(*a), "tensor_tensor": lambda: e.tensor_tensor(*a),
+               "tensor_scalar": lambda: e.tensor_scalar(*a), "tensor_tensor_scan": lambda: e.tensor_tensor_scan(*a),
+               "memset": lambda: e.memset(*a), "tensor_reduce": lambda: e.tensor_reduce(*a),
+               "activation": lambda: e.activation(*a, **k), "matmul": lambda: e.matmul(*a),
+               "iota": lambda: e.iota(*a, **k)}[call]()
+        if i in wanted:
+            s = "s" + q
+            count[s] = count.get(s, 0) + 1
+            ins.then_inc(T.sem[s], 1)
+            mark[i] = (s, count[s])
+    count["out"] = out[0]
+    for s, n in count.items():
+        if known["g"].get(s, 0) < n:
+            g.wait_ge(T.sem[s], n)

@@ -31,16 +31,16 @@ SCRATCH = {
     "bi": _sb(512, I32), "bj": _sb(512, I32), "bk": _sb(512, I32),
     "jg": _sb(128, BF), "bo": _sb(128, BF), "bof": _sb(128, F32), "bo9": _sb(128, BF), "idb": _sb(128, BF), "idf": _sb(128, F32),
     "nid": _sb(128, BF), "it": _sb(128, BF), "nit": _sb(128, BF), "tri": _sb(128, BF), "lt": _sb(128, BF),
-    "jlo": _sb(128, BF), "jhi": _sb(128, BF),
+    "sel": _sb(2048, BF), "jlo": _sb(128, BF), "jhi": _sb(128, BF),
     "gq": _sb(8, F32), "rw": _sb(16, BF), "kr": _sb(128, BF), "kt": _sb(128, BF), "thr": _sb(128, BF), "dth": _sb(96, F32),
     "db": _sb(64, F32), "exi": _sb(16, I32), "exu": _sb(16, U16), "k1": _sb(2, BF), "pw": _sb(64, F32),
     "emp": _sb(512, BF), "s1": _sb(512, BF), "s2": _sb(512, BF), "et": _sb(WIN, BF), "ne": _sb(528, BF),
     "gt": _sb(512, BF), "sg": _sb(512, BF), "cum": _sb(512, BF), "junk": _sb(512, BF), "sm": _sb(16, F32),
     "us": _sb(128, U16), "ue": _sb(24, U16), "ed": _sb(96, F32), "edi": _sb(32, I32), "gb": _sb(96, F32), "df": _sb(96, F32),
     "p1": _sb(352, BF), "p2": _sb(352, BF), "cn": _sb(352, BF), "pr": _sb(352, BF), "ym": _sb(352, BF), "ys": _sb(352, BF),
-    "zz": _sb(176, F32), "ww": _sb(608, BF), "zb": _sb(256, BF), "zo": _sb(256, BF), "gbr": _sb(256, F32),
+    "zz": _sb(208, F32), "ww": _sb(608, BF), "zb": _sb(256, BF), "zo": _sb(256, BF), "gbr": _sb(256, F32),
     "nm": _sb(256, BF), "ns": _sb(256, BF), "dlt": _sb(256, F32), "val": _sb(256, F32), "ax": _sb(256, BF), "aw": _sb(512, BF),
-    "am": _sb(256, BF), "ak": _sb(256, BF),
+    "am": _sb(256, BF),
     "e00": ("sbuf", [128, 8, 128], BF), "e01": ("sbuf", [128, 8, 128], BF), "e11": ("sbuf", [128, 8, 128], BF),
 }
 for _k in range(8):
@@ -105,14 +105,14 @@ def program(rank, T, topo):
             tr.append(RemoteDMATransfer(dst_ids=[DstId(rid=rid, pnc=pid)], dma_engine_mask=sum(1 << e for e in take),
                                         remote_sem=T.sem[sem], src=T[src][r], dst=T[dst][rank]))
             total += len(take)
-        ops.append(("g", "remote", [RAW(src, None), tr, total], {}, 0, ()))
+        ops.append(("g", "remote", [RAW(src, None), tr, total, sem], {}, 0, ()))
 
     def landed(dst, sem):
         ops.append(("x", "landed", [RAW(dst, None), sem, N - 1], {}, 1, ()))
 
     C = {k: col("cc", i) for i, k in enumerate(
         ["pm", "pg", "od", "p32", "p64", "pf", "g512", "b2", "b3", "key", "cb", "ic", "le8", "pw", "x1", "x2", "x3", "x4",
-         "m1", "m2", "m3", "p64h"])}
+         "m1", "m2", "m3", "p64h", "lt8"])}
     D = lambda k: col("diag", k)
 
     ms(A("es", 24, 32), 0)
@@ -156,6 +156,7 @@ def program(rank, T, topo):
     iota(A("kr"), [[32, 4], [1, 2], [2, 16]])
     iota(A("exi"), [[1, 2], [2, 8]])
     iota(A("ww"), [[0, 608]])
+    iota(A("sel"), [[0, 2048]])
     iota(A("lw", 512, 528), [[0, 16]], NV)
     iota(A("lw", 528, WIN), [[0, WIN - 528]])
     iota(A("et"), [[0, WIN]])
@@ -174,6 +175,7 @@ def program(rank, T, topo):
         act(A("tb2", q * V, q * V + V), A("base2"), AF.Identity, bias=col("c2", q))
     ms(A("seg", 0, 1536, 16), 0.0)
     ms(A("k1"), float(K1))
+    ms(A("zz", 176, 192), 0.0)
     ms(A("tt", NV, NV + 16), 0.0)
     ms(A("ne", 512, 528), 2.0 * K1)
     ms(A("nrow", 512, 528), 0.0)
@@ -186,6 +188,7 @@ def program(rank, T, topo):
     ts(C["cb"], C["pm"], 2.0, OP.mult, 1.0, OP.add)
     ts(C["x3"], C["pm"], 8.0, OP.is_ge, 33.0, OP.mult)
     ts(C["le8"], C["pm"], 8.0, OP.is_le)
+    ts(C["lt8"], C["pm"], 8.0, OP.not_equal)
     ts(C["x4"], C["pm"], 2.0, OP.mult, C["od"], OP.add)
     ts(C["p64h"], C["p64"], 64.0, OP.add)
     ts(A("gq"), A("j16", 0, 8), C["pg"], OP.is_equal)
@@ -212,6 +215,8 @@ def program(rank, T, topo):
     ts(A("bo"), A("jg"), C["pg"], OP.is_equal)
     ts(A("bof"), A("jg"), C["pg"], OP.is_equal)
     ts(A("bo9"), A("jg"), C["pg"], OP.is_equal, C["le8"], OP.mult)
+    for r in range(16):
+        tc(A("sel", 128 * r + r, 128 * r + 128, 16), A("bo9", r, 128, 16))
     tt(A("tri"), A("lt"), A("bo"), OP.mult)
     ts(A("kt"), A("kr"), C["key"], OP.is_le, 90.0, OP.mult)
     tc(A("exu"), A("exi"))
@@ -252,6 +257,10 @@ def program(rank, T, topo):
 
     TW, TBW = A("tt"), A("tb")
 
+    def pick(out, name, j0, n):
+        for r in range(16):
+            mm(out, A("sel", 128 * r, 128 * r + 128), A(name, j0 + r, j0 + n, 16), r == 0, r == 15)
+
     def place(j0, n, rec, giv, own32, init, dump, pos, between=lambda: None):
         k = n // 16
         r = lambda name: A(name, j0, j0 + n)
@@ -259,11 +268,9 @@ def program(rank, T, topo):
         act(r("p2"), IND(A("tb2"), giv), AF.Copy)
         scan(r("cn"), r("p1"), A("one", 0, n), init, OP.add, OP.min)
         tt(r("pr"), r("cn"), r("p1"), OP.mult)
-        mm(P(1, 0, n), A("bo9"), r("pr"))
+        y = P(1, 0, k)
+        pick(y, "pr", j0, n)
         between()
-        tt(r("ym"), P(1, 0, n), A("diag", 0, n), OP.mult)
-        scan(r("ys"), A("seg", 0, n), r("ym"), 0.0, OP.mult, OP.add)
-        y = A("ys", j0 + 15, j0 + n, 16)
         tt(A("zz", 0, k), y, dump, OP.mult)
         tt(A("zz", 16, 16 + k), y, own32, OP.add)
         tt(A("zz", 32, 32 + k), A("zz", 0, k), A("zz", 16, 16 + k), OP.max)
@@ -316,7 +323,7 @@ def program(rank, T, topo):
         else:
             act(A("junk", v0, v1), A("cum", v0, v1), AF.Sign, bias=C["cb"], scale=-1.0, acc=col("sm", 0 if v0 == 0 else 4))
 
-    cuts = [[0, 48, 128, 224, 320, 400, 456, 492, 512], [0, 32, 112, 208, 304, 384, 448, 488, 512]]
+    cuts = [[0, 72, 152, 240, 328, 408, 460, 492, 512], [0, 64, 144, 232, 320, 400, 456, 492, 512]]
     for t in range(2):
         last = t == 1
         cut = cuts[t]
@@ -392,12 +399,12 @@ def program(rank, T, topo):
         tc(go, P(1, 16, 32))
         tc(A("zb"), IND(A("bits"), vo))
         act(A("zo"), IND(A("bito"), vo), AF.Copy)
-        tc(A("zz", 48, 64), P(1, 0, 16))
+        tc(A("zz", 192, 208), P(1, 0, 16))
         if not last:
             low(0)
-        units = [("e00", 0, 0, dd, 2 + dd, 0) for dd in range(4)] + [("e01", 0, 1, dd, 6 + dd, 0) for dd in range(2)]
-        units += [("e11", 1, 1, dd, 2 + dd, 256) for dd in range(2)] + [("e01", 0, 1, dd, 4 + dd, 256) for dd in range(2, 4)]
-        units += [("e11", 1, 1, dd, 2 + dd, 256) for dd in range(2, 4)]
+        units = [("e11", 1, 1, dd, 2 + dd, 0) for dd in range(2)] + [("e01", 0, 1, dd, 6 + dd, 0) for dd in range(2)]
+        units += [("e11", 1, 1, dd, 2 + dd, 0) for dd in range(2, 4)] + [("e01", 0, 1, dd, 4 + dd, 256) for dd in range(2, 4)]
+        units += [("e00", 0, 0, dd, 2 + dd, 256) for dd in range(4)]
         for nm, hr, hc, dd, bank, c0 in units:
             for par in range(2):
                 p0 = 32 * dd
@@ -411,24 +418,23 @@ def program(rank, T, topo):
                     tt(o, P(bank, c0 + 128 * par, c0 + 128 * par + 128), A("thr"), OP.is_ge)
                 else:
                     act(o, P(bank, c0 + 128 * par, c0 + 128 * par + 128), AF.Relu, bias=-8.0)
-            if (nm, dd) == ("e00", 0):
+            if (nm, dd) == ("e11", 0):
                 act(A("gbr"), IND(A("iom"), go), AF.Copy)
-        for c in range(8):
-            mm(P(1, 64 + c, 65 + c), RAW("e00", T.e00[:, c, :]), col("k1", 0))
-        for c in range(8):
-            mm(P(1, 72 + c, 73 + c), RAW("e01", T.e01[:, c, :]), col("k1", 0), True, False)
-            mm(P(1, 72 + c, 73 + c), RAW("e11", T.e11[:, c, :]), col("k1", 0), False, True)
         tt(A("nm"), IND(A("ne"), vo), A("diag"), OP.mult)
-        ts(col("sm", 3), col("sm", 2), 512.0, OP.is_ge, C["pm"], OP.mult)
         scan(A("ns"), A("seg", 0, 256), A("nm"), 0.0, OP.mult, OP.add)
-        ts(vsu, col("sm", 3), col("sm", 2), OP.add)
         ts(A("zz", 160, 176), A("ns", 15, 256, 16), -1.0, OP.mult, 2.0 * K1, OP.add)
-        kk = P(1, 64, 80)
-        tt(A("zz", 96, 112), kk, A("zz", 48, 64), OP.add)
-        tt(A("zz", 80, 96), kk, A("zz", 160, 176), OP.is_lt)
-        tt(A("zz", 112, 128), A("zz", 96, 112), A("db", 48, 64), OP.min)
+        mm(P(1, 64, 96), A("idf"), A("zz", 176, 208), True, False)
+        for c in range(8):
+            mm(P(1, 72 + c, 96, 16), RAW("e01", T.e01[:, c, :]), A("k1"), False, False)
+            mm(P(1, 72 + c, 96, 16), RAW("e11", T.e11[:, c, :]), A("k1"), False, False)
+        for c in range(8):
+            mm(P(1, 64 + c, 96, 16), RAW("e00", T.e00[:, c, :]), A("k1"), False, c == 7)
+        ts(col("sm", 3), col("sm", 2), 512.0, OP.is_ge, C["pm"], OP.mult)
+        ts(vsu, col("sm", 3), col("sm", 2), OP.add)
+        tt(A("zz", 112, 128), P(1, 80, 96), A("db", 48, 64), OP.min)
+        tt(A("zz", 80, 96), P(1, 64, 80), A("zz", 160, 176), OP.is_lt)
         act(A("ax"), IND(A("zz", 80, 96), A("exu")), AF.Copy)
-        ts(A("zz", 64, 80), ri, -1.0, OP.mult, float(NV), OP.add)
+        ts(A("zz", 64, 80), ri, -1.0 / 8, OP.mult, NV / 8.0, OP.add)
         ts(off, A("zz", 112, 128), float(NV), OP.add)
         if not last:
             table(0, 6, "a")
@@ -436,6 +442,9 @@ def program(rank, T, topo):
         for s in range(2):
             mm(P(2, s, 256, 2), A("ax", 128 * s, 128 * s + 128), A("idb"))
         act(A("aw", 0, 256), P(2, 0, 256), AF.Copy)
+        act(A("am"), IND(A("aw"), pos), AF.Identity, scale=C["lt8"])
+        pick(P(2, 0, 16), "am", 0, 256)
+        tt(A("zz", 128, 144), P(2, 0, 16), A("zz", 64, 80), OP.mult)
         if not last:
             for q in range(1, 5):
                 table(q, 4 + (q + 2) % 4, "a")
@@ -446,9 +455,6 @@ def program(rank, T, topo):
         if not last:
             for q in range(5, 7):
                 table(q, 4 + (q + 2) % 4, "a")
-        tt(A("am"), IND(A("aw"), pos), A("diag"), OP.mult)
-        scan(A("ak"), A("seg", 0, 256), A("am"), 0.0, OP.mult, OP.add)
-        tt(A("zz", 128, 144), A("ak", 15, 256, 16), A("zz", 64, 80), OP.mult)
         tt(A("zz", 144, 160), IND(LWv, vsu), A("zz", 128, 144), OP.add)
         tc(IND(LWv, vsu), A("zz", 144, 160))
         for v0, v1 in ([(0, 512)] if last else [(0, cuts[1][2]), (cuts[1][2], 512)]):
@@ -482,6 +488,145 @@ def spans(x):
     return [(x[1], x[2], x[3])]
 
 
+def width(x):
+    if x[0] == "ind":
+        return 16 * width(x[2])
+    if x[0] == "raw":
+        return 128
+    return (x[3] - x[2] + x[4] - 1) // x[4]
+
+
+def lasts(op, CYC=0.00095, GAT=1.56, SCA=3.8, PE=0.6, DMA=2.2, FAR=3.5):
+    q, call, args, kw, nout, extra = op
+    if call == "dma_start":
+        return 0.1, DMA
+    if call == "remote":
+        return 1.0, 1.0
+    if call == "landed":
+        return 0.0, FAR
+    n = width(args[0])
+    aps = [x for x in args if isinstance(x, tuple) and x and x[0] in ("ap", "ind", "raw")]
+    two = all(SCRATCH[x[1]][2] in (BF, U16) for x in aps if x[0] != "ind" and width(x) > 1)
+    if call == "matmul":
+        c = PE * max(64, n) * (4 if SCRATCH[args[1][1]][2] == F32 else 1)
+    elif call == "iota":
+        c = 160 + 2 * n
+    elif args[0][0] == "ind":
+        c = 60 + SCA * n
+    elif any(x[0] == "ind" for x in aps):
+        c = 60 + GAT * n
+    elif call == "tensor_tensor":
+        c = max(64, n if any(x[1].endswith("_") for x in aps) else 2 * n)
+    else:
+        c = max(64, n / 2 if two and q == "v" else n)
+    return c * CYC, c * CYC
+
+
+def arrange(ops, deps):
+    n = len(ops)
+    dur = [lasts(o) for o in ops]
+    rest = [0.0] * n
+    for i in range(n - 1, -1, -1):
+        rest[i] += dur[i][1] + HOP
+        for j in deps[i]:
+            rest[j] = max(rest[j], rest[i])
+    start, busy = [0.0] * n, {}
+    for i in sorted(range(n), key=lambda i: (-rest[i], i)):
+        t = max([start[j] + (dur[j][0] if ops[j][0] == ops[i][0] == "p" else dur[j][1] + HOP) for j in deps[i]] + [0.0])
+        for a, b in sorted(busy.get(ops[i][0], [])):
+            if t + dur[i][0] <= a:
+                break
+            t = max(t, b)
+        start[i] = t
+        busy.setdefault(ops[i][0], []).append((t, t + dur[i][0]))
+    return refine(ops, deps, sorted(range(n), key=lambda i: (start[i], -rest[i], i)))
+
+
+def refine(ops, deps, first):
+    n = len(ops)
+    cases = [([lasts(o, *c[:6]) for o in ops], c[6]) for c in CASES]
+    qs = [o[0] for o in ops]
+    kids = [[] for _ in ops]
+    for i in range(n):
+        for j in deps[i]:
+            kids[j].append(i)
+
+    def run(seq, case):
+        dur, hop = cases[case]
+        nxt, left, ready, why = [-1] * n, [len(d) for d in deps], [0.0] * n, [-1] * n
+        for l in seq.values():
+            for a, b in zip(l, l[1:]):
+                nxt[a] = b
+                left[b] += 1
+        todo, order, end, tail = [i for i in range(n) if not left[i]], [], 0.0, -1
+        while todo:
+            i = todo.pop()
+            order.append(i)
+            hold, done = ready[i] + dur[i][0], ready[i] + dur[i][1]
+            if done > end:
+                end, tail = done, i
+            for k in kids[i]:
+                t = hold if qs[i] == qs[k] == "p" else done + hop
+                if t > ready[k]:
+                    ready[k], why[k] = t, i
+                left[k] -= 1
+                if not left[k]:
+                    todo.append(k)
+            k = nxt[i]
+            if k >= 0:
+                if hold > ready[k]:
+                    ready[k], why[k] = hold, i
+                left[k] -= 1
+                if not left[k]:
+                    todo.append(k)
+        if len(order) < n:
+            return 1e9, [], order, ready
+        pairs = []
+        while why[tail] >= 0:
+            if nxt[why[tail]] == tail and why[tail] not in deps[tail]:
+                pairs.append((why[tail], tail))
+            tail = why[tail]
+        return end, pairs, order, ready
+
+    def score(seq):
+        r = [run(seq, c) for c in range(len(cases))]
+        return sum(x[0] / w for x, w in zip(r, WEIGHT)), [p for x in r for p in x[1]]
+
+    seq = {}
+    for i in first:
+        seq.setdefault(qs[i], []).append(i)
+    cur, pairs = score(seq)
+    best, keep, rnd = cur, {q: list(l) for q, l in seq.items()}, 12345
+    for step in range(STEPS):
+        rnd = (rnd * 1103515245 + 12345) % (1 << 31)
+        a, b = pairs[(rnd >> 8) % len(pairs)]
+        l = seq[qs[a]]
+        k = l.index(a)
+        old = list(l)
+        far = (rnd >> 4) % 4
+        if (rnd >> 3) & 1:
+            l.insert(max(0, k - far), l.pop(k + 1))
+        else:
+            l.insert(k + 1 + far, l.pop(k))
+        new, p2 = score(seq)
+        if new <= cur + 0.004 * (1.0 - step / STEPS) * ((rnd >> 12) % 100) / 100.0:
+            cur, pairs = new, p2
+            if cur < best:
+                best, keep = cur, {q: list(x) for q, x in seq.items()}
+        else:
+            seq[qs[a]] = old
+    _, _, order, ready = run(keep, 0)
+    place = {i: k for k, i in enumerate(order)}
+    return sorted(range(n), key=lambda i: (ready[i], place[i]))
+
+
+CASES = [(0.00083, 1.3, 3.0, 0.6, 2.2, 4.0, 0.12), (0.00115, 1.9, 5.0, 0.5, 1.8, 2.5, 0.1)]
+WEIGHT = [85.0, 110.0]
+STEPS = 4000
+HOP = 0.12
+ORDER = []
+
+
 def rank_program(g, core, T, topo):
     rank = T.rank_of(core)
     if rank is None:
@@ -512,22 +657,29 @@ def rank_program(g, core, T, topo):
         dma = call in ("dma_start", "remote", "landed")
         mine = []
         for j, (q2, wr2, rd2, dma2) in enumerate(touch):
-            if q == q2 == "p":
-                continue
             hit = False
             for n, a, b in wr:
                 for n2, a2, b2 in wr2 + rd2:
                     if n == n2 and a < b2 and a2 < b and not (dma and dma2 and (n2, a2, b2) not in rd2):
-                        if not (n.endswith("_") and q == q2 and (n2, a2, b2) not in wr2):
-                            hit = True
+                        hit = True
             for n, a, b in rd:
                 for n2, a2, b2 in wr2 + ([s for s in rd2 if s[0].endswith("_")] if q != q2 else []):
                     if n == n2 and a < b2 and a2 < b:
                         hit = True
-            if hit and call != "landed":
+            if call == "landed":
+                hit = ops[j][1] == "remote" and ops[j][2][3] == args[1]
+            if hit:
                 mine.append(j)
         touch.append((q, wr, rd, dma))
         deps.append(mine)
+    if not ORDER:
+        gp = [i for i, o in enumerate(ops) if o[0] == "g"]
+        after = dict(zip(gp[1:], gp))
+        ORDER.extend(arrange(ops, [d + ([after[i]] if i in after and after[i] not in d else []) for i, d in enumerate(deps)]))
+    order = ORDER
+    place = {i: k for k, i in enumerate(order)}
+    deps = [sorted(place[j] for j in deps[i] if not ops[i][0] == ops[j][0] == "p") for i in order]
+    ops, touch = [ops[i] for i in order], [touch[i] for i in order]
     need = []
     for i, mine in enumerate(deps):
         latest = {}

@@ -6,8 +6,16 @@ NV = N * V
 K1 = 768
 SPARE = K1 + V
 WIN = SPARE + 256
+SEG = 1024
 F32, BF, I32, U16 = "float32", "bfloat16", "int32", "uint16"
 MAGIC = 12582912.0
+
+
+PIECES = [([0, 16, 48, 88, 136], [136, 196, 256], [392, 446, 490, 512], 446)] * 2
+EMPTY, OWNERS, MERGE = "a", "vv", "aa"
+TAB0, TAB1 = "aaavavav", "aaaaaaaa"
+PREP = [0, 128, 256, 512]
+DIAG_ON_SCALAR = [("e11", 1), ("e00", 3)]
 
 
 def _sb(w, d):
@@ -15,38 +23,40 @@ def _sb(w, d):
 
 
 SCRATCH = {
-    "se": ("dram", [8, 128, 4], I32), "sx": ("dram", [8, 128, 64], U16), "sl": ("dram", [8, 128, 64], U16),
-    "le": ("dram", [8, 128, 4], I32), "lx": ("dram", [8, 128, 64], U16), "ll": ("dram", [8, 128, 64], U16),
+    "se": ("dram", [8, 128, 4], I32), "sl": ("dram", [8, 128, 64], U16),
+    "le": ("dram", [8, 128, 4], I32), "ll": ("dram", [8, 128, 64], U16),
     "dx": ("dram", [8, 128, 64], F32), "rx": ("dram", [8, 128, 64], F32),
-    "dl": ("dram", [8, 128, 64], U16), "rl": ("dram", [8, 128, 64], U16),
+    "dl": ("dram", [8, 128, 64], F32), "rl": ("dram", [8, 128, 64], F32),
     "xi": _sb(512, I32), "li": _sb(512, I32), "es": _sb(32, I32), "eu": _sb(32, I32),
     "xs": _sb(512, U16), "ls": _sb(512, U16), "xu": _sb(512, U16), "lu": _sb(512, U16),
-    "ou": _sb(512, U16), "of": _sb(512, F32),
-    "tt": _sb(NV + 16, F32), "gg": _sb(8192, F32), "ms": _sb(8192, F32), "lw": _sb(WIN, F32),
+    "of": _sb(512, F32),
+    "tt": _sb(NV + 16, F32), "gg": _sb(8192, F32), "ms": _sb(8192, F32), "lw": _sb(528, F32),
     "hl": _sb(1024, BF), "a1": _sb(512, F32), "a2": _sb(512, F32), "xo": _sb(512, F32),
-    "rep": _sb(512, BF), "jr": _sb(512, BF), "one": _sb(512, BF), "seg": _sb(1536, BF), "j16": _sb(256, BF), "diag": _sb(256, BF),
-    "iv": _sb(512, F32), "pi": _sb(4, I32), "pt": _sb(8, I32), "cc": _sb(32, F32),
-    "tb": _sb(NV + 16, BF), "tb2": _sb(NV, BF), "iom": _sb(NV, F32), "base": _sb(512, BF), "base2": _sb(512, BF),
-    "c2": _sb(8, F32), "nrow": _sb(528, F32), "bits": _sb(528, BF), "bito": _sb(528, BF),
+    "rep": _sb(512, BF), "jr": _sb(512, BF), "one": _sb(512, BF), "seg": _sb(SEG, BF), "j16": _sb(256, BF), "diag": _sb(256, BF),
+    "iv": _sb(512, F32), "pi": _sb(4, I32), "pt": _sb(8, I32), "cc": _sb(40, F32),
+    "tb": _sb(NV + 16, BF), "iom": _sb(NV, F32), "base": _sb(512, BF),
+    "c2": _sb(16, F32), "nrow": _sb(528, F32), "bits": _sb(528, BF), "bito": _sb(528, BF),
     "bi": _sb(512, I32), "bj": _sb(512, I32), "bk": _sb(512, I32),
-    "jg": _sb(128, BF), "bo": _sb(128, BF), "bof": _sb(128, F32), "bo9": _sb(128, BF), "idb": _sb(128, BF), "idf": _sb(128, F32),
+    "jg": _sb(128, BF), "bo": _sb(128, BF), "bof": _sb(128, F32), "idb": _sb(128, BF), "idf": _sb(128, F32),
     "nid": _sb(128, BF), "it": _sb(128, BF), "nit": _sb(128, BF), "tri": _sb(128, BF), "lt": _sb(128, BF),
-    "sel": _sb(2048, BF), "jlo": _sb(128, BF), "jhi": _sb(128, BF),
+    "sel": _sb(144, BF), "turn": _sb(512, F32), "j64": _sb(64, BF), "lp": _sb(512, U16), "jlo": _sb(128, BF), "jhi": _sb(128, BF),
     "gq": _sb(8, F32), "rw": _sb(16, BF), "kr": _sb(128, BF), "kt": _sb(128, BF), "thr": _sb(128, BF), "dth": _sb(96, F32),
-    "db": _sb(64, F32), "exi": _sb(16, I32), "exu": _sb(16, U16), "k1": _sb(2, BF), "pw": _sb(64, F32),
-    "emp": _sb(512, BF), "s1": _sb(512, BF), "s2": _sb(512, BF), "et": _sb(WIN, BF), "ne": _sb(528, BF),
+    "db": _sb(64, F32), "k1": _sb(2, BF), "pw": _sb(64, F32), "c33": _sb(256, BF), "c32": _sb(16, BF), "q4": _sb(128, BF),
+    "rep0": _sb(512, BF), "band": _sb(960, BF), "bitc": _sb(512, BF), "nb16": _sb(128, BF), "s10": _sb(128, BF), "s9": _sb(128, BF),
+    "r910": _sb(128, BF), "msk": _sb(128, BF),
+    "emp": _sb(512, BF), "et": _sb(WIN, BF), "dw": _sb(WIN, F32),
     "gt": _sb(512, BF), "sg": _sb(512, BF), "cum": _sb(512, BF), "junk": _sb(512, BF), "sm": _sb(16, F32),
     "us": _sb(128, U16), "ue": _sb(24, U16), "ed": _sb(96, F32), "edi": _sb(32, I32), "gb": _sb(96, F32), "df": _sb(96, F32),
     "p1": _sb(352, BF), "p2": _sb(352, BF), "cn": _sb(352, BF), "pr": _sb(352, BF), "ym": _sb(352, BF), "ys": _sb(352, BF),
-    "zz": _sb(208, F32), "ww": _sb(608, BF), "zb": _sb(256, BF), "zo": _sb(256, BF), "gbr": _sb(256, F32),
-    "nm": _sb(256, BF), "ns": _sb(256, BF), "dlt": _sb(256, F32), "val": _sb(256, F32), "ax": _sb(256, BF), "aw": _sb(512, BF),
+    "zz": _sb(208, F32), "ze": _sb(48, F32), "ww": _sb(608, BF), "zb": _sb(256, BF), "zo": _sb(256, BF), "gbr": _sb(256, F32),
+    "nm": _sb(256, BF), "ns": _sb(256, BF), "dlt": _sb(256, F32), "ax": _sb(256, BF), "aw": _sb(512, BF),
     "am": _sb(256, BF),
     "e00": ("sbuf", [128, 8, 128], BF), "e01": ("sbuf", [128, 8, 128], BF), "e11": ("sbuf", [128, 8, 128], BF),
 }
 for _k in range(8):
     SCRATCH["p%d_" % _k] = ("psum", [128, 512], F32)
 NDMA = 24
-SEMAPHORES = ["sv", "sa", "sp", "sg", "ae", "ax", "al", "bx", "bl", "out"] + ["d%d" % k for k in range(NDMA)]
+SEMAPHORES = ["sv", "sa", "sp", "sg", "ae", "ax", "al", "bx", "bl", "out", "in"] + ["d%d" % k for k in range(NDMA)]
 
 
 def program(rank, T, topo):
@@ -84,10 +94,11 @@ def program(rank, T, topo):
         if scale is not None: kw["scale"] = scale
         if acc is not None: kw["accum_out"] = acc
         put("a", "activation", [out, in_, f], kw, 1, (acc,) if acc is not None else ())
+    def lin(out, in_, scale=None, bias=None): act(out, in_, AF.Identity, bias, scale)
     def mm(out, l, r, st=True, sp=True): put("p", "matmul", [out, l, r, st, sp])
     def iota(out, pat, base=0, cm=0):
         put("g", "iota", [out, pat, base, cm], {} if SCRATCH[out[1]][2] == I32 else {"allow_small_or_imprecise_dtypes": True})
-    def dma(q, out, in_): put(q, "dma_start", [out, in_])
+    def dma(q, out, in_, shared=None): put(q, "dma_start", [out, in_] + ([shared] if shared else []))
 
     me = T.cores[rank]
     own = dict(p0=16 * rank, p1=16 * rank + 16)
@@ -95,6 +106,9 @@ def program(rank, T, topo):
     def exchange(buf, src, dst, sem, q2="s"):
         dma("s", RAW(src, T[src][:]), A(buf))
         dma(q2, RAW(dst, T[dst][rank]), A(buf, **own))
+        send(src, lambda r: T[src][r], T[dst][rank], sem)
+
+    def send(src, piece, slot, sem):
         far = [r for r in range(N) if r != rank and topo.chip(T.cores[r]) != topo.chip(me)]
         used, tr, total = set(), [], 0
         for r in far + [r for r in range(N) if r != rank and r not in far]:
@@ -103,7 +117,7 @@ def program(rank, T, topo):
             used.update(take)
             rid, pid, _ = topo.addr(T.cores[r])
             tr.append(RemoteDMATransfer(dst_ids=[DstId(rid=rid, pnc=pid)], dma_engine_mask=sum(1 << e for e in take),
-                                        remote_sem=T.sem[sem], src=T[src][r], dst=T[dst][rank]))
+                                        remote_sem=T.sem[sem], src=piece(r), dst=slot))
             total += len(take)
         ops.append(("g", "remote", [RAW(src, None), tr, total, sem], {}, 0, ()))
 
@@ -112,18 +126,26 @@ def program(rank, T, topo):
 
     C = {k: col("cc", i) for i, k in enumerate(
         ["pm", "pg", "od", "p32", "p64", "pf", "g512", "b2", "b3", "key", "cb", "ic", "le8", "pw", "x1", "x2", "x3", "x4",
-         "m1", "m2", "m3", "p64h", "lt8"])}
+         "m1", "m2", "m3", "p64h", "lo", "hi", "t16", "x0", "g15", "d9", "ma", "mb", "d13", "y1", "y2"])}
     D = lambda k: col("diag", k)
 
     ms(A("es", 24, 32), 0)
-    dma("s", A("xi"), RAW("x0", T.x0[:]))
+    dma("a", A("li"), RAW("l0", T.l0[:]))
+    for r in range(N):
+        for h in range(2):
+            dma("sa"[h], A("xi", 64 * r, 64 * r + 64, 1, 64 * h, 64 * h + 64),
+                RAW("x0", T.x0[16 * r:16 * r + 16, 256 * h:256 * h + 256]), "in")
     dma("a", A("es", 0, 12), RAW("ea", T.ea[:]))
     dma("s", A("es", 12, 24), RAW("eb", T.eb[:]))
     dma("a", A("es", 24, 26), RAW("u", T.u[:]))
-    dma("a", A("li"), RAW("l0", T.l0[:]))
     iota(col("pi", 0), [[0, 1]], 0, 1)
     iota(A("j16"), [[0, 16], [1, 16]])
     iota(A("iv"), [[1, 512]])
+    tc(A("ls"), A("li"))
+    tc(A("xs"), A("xi"))
+    tc(RAW("xu", T.xu[:, 64 * rank:64 * rank + 64]), RAW("xs", T.xs[:, 64 * rank:64 * rank + 64]))
+    send("xs", lambda r: T.xs[:, 64 * r:64 * r + 64], T.xu[:, 64 * rank:64 * rank + 64], "ax")
+    exchange("ls", "sl", "ll", "al")
     exchange("es", "se", "le", "ae", "a")
     ms(A("pw", 0, 16), 0.5)
     ms(A("pw", 16, 32), 0.0)
@@ -139,28 +161,33 @@ def program(rank, T, topo):
     ms(A("one"), 1.0)
     ms(A("pw", 41, 45, 2), 1.0 / 64)
     ts(A("diag"), A("j16"), C["pm"], OP.is_equal)
-    ts(C["g512"], C["pg"], 512.0, OP.mult)
+    lin(C["g512"], C["pg"], 512.0)
     tt(A("pw", 48, 64), A("pw", 32, 48), A("diag", 0, 16), OP.mult)
-    ts(C["m1"], D(9), D(10), OP.add)
-    ts(C["m2"], D(9), -64.0, OP.mult)
     put("v", "tensor_reduce", [C["pw"], A("pw", 48, 64), AxisListType.X, OP.add])
-    ts(C["m3"], D(11), D(12), OP.add)
-    ts(A("c2"), A("j16", 0, 8), 8.0, OP.mult, D(11), OP.mult)
+    lin(C["x0"], D(9), 1.0, D(10))
+    lin(C["m3"], D(11), 1.0, D(12))
+    lin(C["m1"], C["x0"], 1.0 / 64, C["m3"])
+    lin(C["m2"], D(9), -1.0)
+    lin(C["mb"], C["m3"], 1.0, D(13))
+    lin(C["ma"], C["mb"], -1.0, 1.0)
+    lin(C["d13"], D(13))
+    lin(A("c2", 8, 16), A("j16", 0, 8), C["d13"])
+    tt(A("c2", 0, 8), A("c2", 8, 16), A("diag", 0, 8), OP.add)
     act(A("a1"), A("iv"), AF.Identity, bias=-0.499, scale=C["pw"])
-    tc(A("xs"), A("xi"))
-    exchange("xs", "sx", "lx", "ax")
-    tc(A("ls"), A("li"))
-    exchange("ls", "sl", "ll", "al")
     iota(A("jr"), [[16, 4], [0, 8], [1, 16]])
+    iota(A("rep0"), [[1, 4], [0, 8], [4, 16]])
+    iota(A("band"), [[1, 4], [4, 240]], -448)
     iota(A("jg"), [[1, 8], [0, 16]])
     iota(A("kr"), [[32, 4], [1, 2], [2, 16]])
-    iota(A("exi"), [[1, 2], [2, 8]])
     iota(A("ww"), [[0, 608]])
-    iota(A("sel"), [[0, 2048]])
+    iota(A("j64"), [[16, 8], [1, 8]])
+    iota(A("turn"), [[0, 512]])
     iota(A("lw", 512, 528), [[0, 16]], NV)
-    iota(A("lw", 528, WIN), [[0, WIN - 528]])
+    iota(A("c33"), [[0, 256]], 33)
+    iota(A("dw"), [[0, WIN]])
     iota(A("et"), [[0, WIN]])
     iota(A("aw"), [[0, 512]])
+    iota(A("ax"), [[0, 256]])
     iota(A("iom"), [[1, NV]], -NV)
 
     tc(A("bi"), A("a1"))
@@ -168,71 +195,87 @@ def program(rank, T, topo):
     ts(A("bk"), A("bi"), 63, OP.bitwise_and)
     ts(A("bj"), A("bi"), 1, OP.bitwise_and)
     ts(A("base"), A("bk"), C["m1"], OP.mult, C["m2"], OP.add)
-    ts(A("base2"), A("bk"), C["m3"], OP.mult)
     for q in range(N):
-        act(A("tb", q * V, q * V + V), A("base"), AF.Identity, bias=D(q))
-    for q in range(N):
-        act(A("tb2", q * V, q * V + V), A("base2"), AF.Identity, bias=col("c2", q))
-    ms(A("seg", 0, 1536, 16), 0.0)
-    ms(A("k1"), float(K1))
+        act(A("tb", q * V, q * V + V), A("base"), AF.Identity, bias=col("c2", q))
+    ms(A("seg", 0, SEG, 16), 0.0)
+    ms(A("k1", 0, 1), 1.0)
+    ms(A("k1", 1, 2), float(K1))
+    ms(A("c32"), 32.0)
+    ms(A("q4"), -1.0 / 256)
     ms(A("zz", 176, 192), 0.0)
     ms(A("tt", NV, NV + 16), 0.0)
-    ms(A("ne", 512, 528), 2.0 * K1)
     ms(A("nrow", 512, 528), 0.0)
     ms(A("bits", 512, 528), 0.0)
     ms(A("bito", 512, 528), 0.0)
-    ts(C["x1"], D(9), 64.0, OP.mult, D(10), OP.add)
-    ts(C["x2"], D(11), 64.0, OP.mult, D(12), OP.add)
-    ts(C["b2"], C["pm"], 9.0, OP.is_lt, 2.0, OP.mult)
-    ts(C["b3"], C["pm"], 9.0, OP.is_lt, -1.0, OP.mult)
-    ts(C["cb"], C["pm"], 2.0, OP.mult, 1.0, OP.add)
-    ts(C["x3"], C["pm"], 8.0, OP.is_ge, 33.0, OP.mult)
-    ts(C["le8"], C["pm"], 8.0, OP.is_le)
-    ts(C["lt8"], C["pm"], 8.0, OP.not_equal)
-    ts(C["x4"], C["pm"], 2.0, OP.mult, C["od"], OP.add)
-    ts(C["p64h"], C["p64"], 64.0, OP.add)
+    lin(C["y1"], D(9), 64.0, D(10))
+    lin(C["x1"], C["y1"], 64.0)
+    lin(C["y2"], D(11), 64.0, D(12))
+    lin(C["x2"], D(13), 512.0, C["y2"])
+    act(C["le8"], C["pm"], AF.Sign, bias=8.5, scale=-1.0)
+    lin(C["b2"], C["le8"], 1.0, 1.0)
+    lin(C["b3"], C["b2"], -0.5)
+    lin(C["le8"], C["b2"], 0.5)
+    lin(C["cb"], C["pm"], 2.0, 1.0)
+    ts(C["ic"], C["pm"], 8.0, OP.is_ge, 33.0, OP.mult)
+    lin(C["lo"], D(10), 4.0, C["b3"])
+    lin(C["x3"], D(10), 15.0, C["le8"])
+    lin(C["hi"], D(9), 2.0, C["x3"])
+    lin(C["t16"], D(10), 16.0)
+    lin(C["x4"], C["pm"], 2.0, C["od"])
+    lin(C["p64h"], C["p64"], 1.0, 64.0)
     ts(A("gq"), A("j16", 0, 8), C["pg"], OP.is_equal)
-    ts(A("db", 0, 16), A("j16", 0, 16), 16.0, OP.mult, C["pm"], OP.add)
-    ts(A("dth"), A("diag", 0, 96), -1.0, OP.add, 1.0e7, OP.mult)
-    ts(C["ic"], C["x3"], -32.0, OP.add)
-    ts(C["key"], C["x4"], C["p32"], OP.add)
-    ts(A("rw", 0, 8), A("gq"), C["x1"], OP.mult)
-    ts(A("rw", 8, 16), A("gq"), C["x2"], OP.mult)
-    ts(A("db", 16, 32), A("db", 0, 16), 256.0 - 31, OP.add)
-    ts(A("db", 32, 48), A("db", 0, 16), 512.0 - 31, OP.add)
-    ts(A("db", 48, 64), A("db", 0, 16), float(SPARE - NV), OP.add)
-    ts(A("tb", NV, NV + 16), A("one", 0, 16), D(8), OP.mult)
+    lin(A("db", 0, 16), A("j16", 0, 16), 16.0, C["pm"])
+    lin(A("dth"), A("diag", 0, 96), 1.0e7, -1.0e7)
+    lin(C["key"], C["x4"], 1.0, C["p32"])
+    lin(A("rw", 0, 8), A("gq"), C["x1"])
+    lin(A("rw", 8, 16), A("gq"), C["x2"])
+    lin(A("db", 16, 32), A("db", 0, 16), 1.0, 256.0 - 31)
+    lin(A("db", 32, 48), A("db", 0, 16), 1.0, 512.0 - 31)
+    lin(A("db", 48, 64), A("db", 0, 16), 1.0, float(SPARE - NV))
+    lin(A("tb", NV, NV + 16), A("one", 0, 16), 0.0, D(8))
     ts(A("idb"), A("iv", 0, 128), C["pf"], OP.is_equal)
-    ts(A("nid"), A("iv", 0, 128), C["pf"], OP.is_equal, -1.0, OP.mult)
-    ts(A("lt"), A("iv", 0, 128), C["pf"], OP.is_gt)
-    ts(A("idf"), A("iv", 0, 128), C["pf"], OP.is_equal)
+    lin(A("nid"), A("idb"), -1.0)
+    lin(A("idf"), A("idb"))
     ts(A("jlo"), A("iv", 0, 128), C["p64"], OP.is_equal)
     ts(A("jhi"), A("iv", 0, 128), C["p64h"], OP.is_equal)
-    ts(A("bits", 0, 512), A("bj"), C["b2"], OP.mult, C["b3"], OP.add)
-    ts(A("nrow", 0, 512), A("iv"), C["g512"], OP.add)
-    ts(A("bito", 0, 512), A("bits", 0, 512), C["od"], OP.mult)
-    ts(A("rep"), A("jr"), C["p64"], OP.is_equal)
+    ts(A("bitc"), A("bj"), C["b2"], OP.mult, C["b3"], OP.add)
+    lin(A("nrow", 0, 512), A("iv"), 1.0, C["g512"])
+    lin(A("bito", 0, 512), A("bitc"), C["od"])
     ts(A("bo"), A("jg"), C["pg"], OP.is_equal)
-    ts(A("bof"), A("jg"), C["pg"], OP.is_equal)
-    ts(A("bo9"), A("jg"), C["pg"], OP.is_equal, C["le8"], OP.mult)
-    for r in range(16):
-        tc(A("sel", 128 * r + r, 128 * r + 128, 16), A("bo9", r, 128, 16))
+    lin(A("bof"), A("bo"))
+    lin(A("nb16"), A("bo"), -16.0)
+    lin(A("s10"), A("bo"), C["t16"])
+    lin(C["d9"], D(9))
+    lin(A("s9"), A("bo"), C["d9"])
+    ts(A("r910"), A("j16", 0, 128), 9.0, OP.is_ge)
+    ts(A("lt"), A("j16", 0, 128), 10.0, OP.is_le)
+    tt(A("kt"), A("r910"), A("lt"), OP.mult)
+    ts(A("rep"), A("jr"), C["p64"], OP.is_equal)
+    ts(A("rep0"), A("rep0"), C["p64"], OP.is_equal)
+    ts(A("band"), A("band"), C["p64"], OP.is_equal)
+    for h in range(2):
+        for b in range(2):
+            ts(A("turn", 256 * h + 128 * b + b, 256 * h + 128 * b + 128, 2), A("j64"), 8.0 * h, OP.add, C["pf"], OP.is_equal)
+    lin(C["g15"], C["pg"], 16.0, 15.0)
+    ts(A("sel"), A("iv", 0, 144), C["g15"], OP.is_equal, C["le8"], OP.mult)
+    tt(A("r910"), A("kt"), A("bo"), OP.mult)
+    ts(A("lt"), A("iv", 0, 128), C["pf"], OP.is_gt)
     tt(A("tri"), A("lt"), A("bo"), OP.mult)
-    ts(A("kt"), A("kr"), C["key"], OP.is_le, 90.0, OP.mult)
-    tc(A("exu"), A("exi"))
+    ts(A("msk"), A("kr"), C["key"], OP.is_le, -16.0, OP.mult)
     tt(A("it"), A("idb"), A("tri"), OP.subtract)
-    tt(A("nit"), A("tri"), A("idb"), OP.subtract)
-    ts(A("thr"), A("kt"), 9.0, OP.add)
+    lin(A("nit"), A("it"), -1.0)
+    lin(A("thr"), A("msk"), -1.0, 9.0)
 
+    landed("xu", "ax")
     landed("le", "ae")
     dma("s", A("eu"), RAW("le", T.le[:]))
-    landed("lx", "ax")
-    dma("s", A("xu"), RAW("lx", T.lx[:]))
     landed("ll", "al")
     dma("s", A("lu"), RAW("ll", T.ll[:]))
+    for h in range(2):
+        dma("as"[h], A("lp", 256 * h, 256 * h + 256), RAW("ll", T.ll[:, 64 * h:64 * h + 64, :]))
     ts(A("ed", 0, 12), A("eu", 0, 12), C["g512"], OP.add)
     tc(A("ed", 12, 24), A("eu", 12, 24))
-    ts(A("sm", 8, 10), A("eu", 24, 26), -0.25, OP.add)
+    ts(A("sm", 10, 12), A("eu", 24, 26), -1.0, OP.mult, 65535.0, OP.add)
     tc(A("ue"), A("ed", 0, 24))
     tt(A("ed", 24, 36), A("ed", 0, 12), A("ed", 12, 24), OP.subtract)
 
@@ -248,42 +291,65 @@ def program(rank, T, topo):
         else:
             tc(A("tt", q * V, q * V + V), P(bank))
 
-    tc(P(0), A("xu"))
-    for h in range(2):
-        ts(HL(h, h), A("xu", p0=64 * h, p1=64 * h + 64), 1.0, OP.mult)
-        low(h)
-    for q in range(8):
-        table(q, 2 + q % 6, "v" if q in (3, 5, 7) else "a")
+    landing = [(q, h, k) for q in range(N) for h in range(2) for k in range(4)]
+    came = lambda q, h: A("hl", 512 * h + 64 * q, 512 * h + 64 * q + 64)
+    for c0, c1 in zip(PREP, PREP[1:]):
+        part = lambda h, up: A("hl", 512 * h + c0, 512 * h + c1, 1, 64 * up, 64 * up + 64)
+        tc(P(1, c0, c1), A("xu", c0, c1))
+        for h in range(2):
+            ts(part(h, h), A("xu", c0, c1, 1, 64 * h, 64 * h + 64), 1.0, OP.mult)
+            tt(part(h, 1 - h), P(1, c0, c1, 1, 64 * h, 64 * h + 64), part(h, h), OP.subtract)
+    for q, h, k in landing:
+        bank = 2 + q % 6
+        mm(P(bank, 256 * h + 64 * k, 256 * h + 64 * k + 64), A("rep0", 128 * k, 128 * k + 128), came(q, h))
+        if (h, k) == (1, 3):
+            if TAB0[q] == "a":
+                act(A("tt", q * V, q * V + V), P(bank), AF.Copy)
+            else:
+                tc(A("tt", q * V, q * V + V), P(bank))
+
+    def own_values(bank, close):
+        for q, h, k in landing:
+            c = 240 * k + 112 - 16 * q
+            mm(P(bank, 256 * h + 64 * k, 256 * h + 64 * k + 64), A("band", c, c + 128), came(q, h), False, close and (q, h, k) == landing[-1])
+
+    mm(P(0), A("ax", 0, 128), A("one"), True, False)
+    own_values(0, True)
 
     TW, TBW = A("tt"), A("tb")
 
-    def pick(out, name, j0, n):
+    def pick(out, name, j0, n, first=True):
         for r in range(16):
-            mm(out, A("sel", 128 * r, 128 * r + 128), A(name, j0 + r, j0 + n, 16), r == 0, r == 15)
+            mm(out, A("sel", 15 - r, 143 - r), A(name, j0 + r, j0 + n, 16), first and r == 0, r == 15)
 
     def place(j0, n, rec, giv, own32, init, dump, pos, between=lambda: None):
         k = n // 16
         r = lambda name: A(name, j0, j0 + n)
-        tc(r("p1"), IND(TBW, rec))
-        act(r("p2"), IND(A("tb2"), giv), AF.Copy)
-        scan(r("cn"), r("p1"), A("one", 0, n), init, OP.add, OP.min)
-        tt(r("pr"), r("cn"), r("p1"), OP.mult)
-        y = P(1, 0, k)
-        pick(y, "pr", j0, n)
+        if j0 or OWNERS[t] == "a":
+            lin(r("p1"), IND(TBW, rec), C["ma"])
+        else:
+            ts(r("p1"), IND(TBW, rec), C["ma"], OP.mult)
+        lin(r("p2"), IND(TBW, giv), C["mb"])
+        scan(r("cn"), r("p1"), A("c33", 0, n), init, OP.add, OP.min)
+        scan(r("pr"), r("cn"), r("p1"), 0.0, OP.max, OP.mult)
+        y = P(6 if j0 else 1, 0, k)
+        mm(y, A("nid"), A("c32", 0, k), True, False)
+        pick(y, "pr", j0, n, False)
         between()
-        tt(A("zz", 0, k), y, dump, OP.mult)
-        tt(A("zz", 16, 16 + k), y, own32, OP.add)
-        tt(A("zz", 32, 32 + k), A("zz", 0, k), A("zz", 16, 16 + k), OP.max)
-        ts(pos, A("zz", 32, 32 + k), 31.0, OP.add)
+        z = lambda c: A("ze" if j0 else "zz", c, c + k)
+        tt(z(0), y, dump, OP.mult)
+        tt(z(16), y, own32, OP.add)
+        tt(z(32), z(0), z(16), OP.max)
+        ts(pos, z(32), 31.0, OP.add)
         tt(IND(A("ww"), pos), r("p1"), r("p2"), OP.add)
 
     def edges(t):
         c = 6 * t
-        tc(A("gb"), IND(TW, A("ue", 12 + c, 18 + c)))
+        act(A("gb"), IND(TW, A("ue", 12 + c, 18 + c)), AF.Copy)
         tt(A("df"), IND(TW, A("ue", c, c + 6)), A("gb"), OP.subtract)
-        mm(P(1, 0, B), A("bof"), A("df"))
+        mm(P(6, 0, B), A("bof"), A("df"))
         yield
-        tt(A("ym", 256, 352), P(1, 0, B), A("dth"), OP.is_le)
+        tt(A("ym", 256, 352), P(6, 0, B), A("dth"), OP.is_le)
         scan(A("ys", 256, 352), A("seg", 0, B), A("ym", 256, 352), 0.0, OP.mult, OP.add)
         tt(A("ed", 48, 54), A("ys", 256 + 15, 352, 16), A("ed", 24 + c, 30 + c), OP.mult)
         tt(A("edi", 0, 6), A("ed", 48, 54), A("ed", 12 + c, 18 + c), OP.add)
@@ -304,18 +370,24 @@ def program(rank, T, topo):
     def top(v0, v1):
         scan(A("ms", 16 * v0, 16 * v1), A("seg", 0, 16 * (v1 - v0)), A("gg", 16 * v0, 16 * v1), 0.0, OP.mult, OP.max)
 
+    def paired(c0, c1):
+        a, b = A("gg", 16 * c0, 16 * c1), A("gg", 4096 + 16 * c0, 4096 + 16 * c1)
+        act(a, IND(TW, A("lp", c0, c1)), AF.Copy)
+        tt(b, IND(TW, A("lp", 256 + c0, 256 + c1)), a, OP.max)
+        for h in range(2):
+            scan(A("ms", 4096 * h + 16 * c0 + 1, 4096 * h + 16 * c1, 2), A("seg", 0, 16 * (c1 - c0), 2),
+                 A("gg", 4096 + 16 * c0 + h, 4096 + 16 * c1, 2), 0.0, OP.mult, OP.max)
+
     def M(v0, v1):
         return A("ms", 16 * v0 + 15, 16 * v1, 16)
 
     def ripe(v0, v1, part):
         if part == 0:
             tt(A("gt", v0, v1), P(0, v0, v1), M(v0, v1), OP.is_gt)
-            mm(P(2, v0, v1), A("idb"), A("s1", v0, v1), True, False)
-            mm(P(2, v0, v1), A("nid"), A("s2", v0, v1), False, False)
+            mm(P(2, v0, v1), A("s10"), A("bits", v0, v1), True, False)
+            mm(P(2, v0, v1), A("nb16"), A("emp", v0, v1), False, False)
             mm(P(2, v0, v1), A("bo"), A("gt", v0, v1), False, True)
-            mm(P(4, v0, v1), A("jlo"), A("hl", v0, v1), True, False)
-            mm(P(4, v0, v1), A("jhi"), A("hl", 512 + v0, 512 + v1), False, False)
-            mm(P(4, v0, v1), A("idf"), M(v0, v1), False, True)
+            mm(P(4, v0, v1), A("idf"), M(v0, v1), False, v1 == V)
         elif part == 1:
             act(A("sg", v0, v1), P(2, v0, v1), AF.Sign, bias=-11.5)
         elif part == 2:
@@ -323,43 +395,35 @@ def program(rank, T, topo):
         else:
             act(A("junk", v0, v1), A("cum", v0, v1), AF.Sign, bias=C["cb"], scale=-1.0, acc=col("sm", 0 if v0 == 0 else 4))
 
-    cuts = [[0, 72, 152, 240, 328, 408, 460, 492, 512], [0, 64, 144, 232, 320, 400, 456, 492, 512]]
     for t in range(2):
         last = t == 1
-        cut = cuts[t]
-        RA = cut[5]
-        e = edges(t)
-        gather("a", cut[1], cut[2])
-        next(e)
+        pairs, low_, high, RA = PIECES[t]
+        for _ in edges(t):
+            pass
         if t == 0:
             tc(A("lw", 0, 512), A("lu"))
-        ts(A("emp"), A("lu"), float(NV), OP.is_equal)
-        mm(P(3), A("bo"), A("emp"))
-        next(e)
-        gather("a", cut[2], cut[3])
-        gather("v", cut[0], cut[1])
-        top(cut[0], cut[1])
-        top(cut[1], cut[2])
-        act(A("s1"), P(3), AF.Relu, bias=48.0, scale=-12.0)
-        act(A("s2"), P(3), AF.Relu, bias=-255.0, scale=17.0)
-        next(e, None)
-        mm(P(5), A("bo"), A("emp"))
+            ts(A("emp"), A("lu"), float(NV), OP.is_equal)
+        elif EMPTY == "v":
+            ts(A("emp"), A("lw", 0, 512), float(NV), OP.is_equal)
+        else:
+            act(A("emp"), A("lw", 0, 512), AF.Relu, bias=1.0 - NV)
+        mm(P(5), A("idb"), A("bitc"), True, False)
+        mm(P(5), A("r910"), A("emp"), False, True)
+        ts(A("bits", 0, 512), P(5), C["lo"], OP.max, C["hi"], OP.min)
         mm(P(3), A("it"), A("emp"))
-        gather("a", cut[3], cut[4])
-        top(cut[2], cut[3])
-        gather("a", cut[4], cut[5])
-        top(cut[3], cut[4])
-        gather("a", cut[5], cut[6])
-        top(cut[4], cut[5])
-        ripe(0, RA, 0)
-        gather("a", cut[6], cut[7])
-        top(cut[5], cut[6])
-        gather("a", cut[7], cut[8])
-        ripe(0, RA, 1)
-        top(cut[6], cut[7])
-        ripe(0, RA, 2)
-        ripe(0, RA, 3)
-        top(cut[7], cut[8])
+        mm(P(4), A("q4"), A("one"), True, False)
+        if t == 0:
+            own_values(4, False)
+        else:
+            mm(P(4), A("jlo"), A("hl", 0, V), False, False)
+            mm(P(4), A("jhi"), A("hl", V, 2 * V), False, False)
+        for c0, c1 in zip(pairs, pairs[1:]):
+            paired(c0, c1)
+        for v0, v1 in list(zip(low_, low_[1:])) + list(zip(high, high[1:])):
+            gather("a", v0, v1)
+            top(v0, v1)
+        for k in range(4):
+            ripe(0, RA, k)
         ripe(RA, 512, 0)
         ts(col("sm", 1), col("sm", 0), 0.5, OP.mult, 256.0, OP.add)
         act(A("et", 0, 512), P(3), AF.Relu)
@@ -367,7 +431,8 @@ def program(rank, T, topo):
             ripe(RA, 512, k)
         vs, vsu = A("us", 32, 33), A("us", 34, 35)
         ts(vs, col("sm", 4), 0.5, OP.mult, col("sm", 1), OP.add)
-        act(A("a1"), P(4), AF.Relu, bias=col("sm", 8 + t), scale=0.5)
+        act(A("a2"), P(4), AF.Relu, bias=col("sm", 10 + t), scale=-0.5)
+        act(A("a1"), A("a2"), AF.Identity, bias=MAGIC + 65535.0, scale=-1.0)
         mm(P(3), A("it"), A("emp"), True, False)
         mm(P(3), A("nit"), A("et", 0, 512), False, True)
         LWv = A("lw", 0, 528)
@@ -379,16 +444,14 @@ def program(rank, T, topo):
             tc(A("edi", 16, 32), ri)
             ts(col("sm", 2), col("sm", 4), 0.5, OP.mult, col("sm", 1), OP.add)
             ts(A("edi", 16, 32), A("edi", 16, 32), 4, OP.arith_shift_right, 0xE0, OP.bitwise_and)
-            act(A("a2"), A("a1"), AF.Identity, bias=MAGIC + 65535.0, scale=-1.0)
-            act(A("a1"), A("a2"), AF.Relu, bias=-MAGIC)
+            tc(A("zz", 64, 80), ri)
             if last:
-                act(A("xo"), A("a1"), AF.Identity, bias=65535.0, scale=-1.0)
+                act(A("xo"), A("a1"), AF.Relu, bias=-MAGIC)
                 exchange("xo", "dx", "rx", "bx")
             else:
-                act(P(0), A("a1"), AF.Identity, bias=65535.0, scale=-1.0)
+                act(P(0), A("a1"), AF.Relu, bias=-MAGIC)
                 for h in range(2):
-                    act(HL(h, h), A("a1", p0=64 * h, p1=64 * h + 64), AF.Identity, bias=65535.0, scale=-1.0)
-            act(A("ne", 0, 512), P(5), AF.Relu, bias=2.0 * K1, scale=-float(K1))
+                    act(HL(h, h), A("a1", p0=64 * h, p1=64 * h + 64), AF.Relu, bias=-MAGIC)
             act(A("et", K1, K1 + V), P(3), AF.Relu)
 
         place(0, 256, ri, gi, A("edi", 16, 32), col("cn", 351), A("db", 16, 32), pos, between)
@@ -401,28 +464,35 @@ def program(rank, T, topo):
         act(A("zo"), IND(A("bito"), vo), AF.Copy)
         tc(A("zz", 192, 208), P(1, 0, 16))
         if not last:
-            low(0)
-        units = [("e11", 1, 1, dd, 2 + dd, 0) for dd in range(2)] + [("e01", 0, 1, dd, 6 + dd, 0) for dd in range(2)]
-        units += [("e11", 1, 1, dd, 2 + dd, 0) for dd in range(2, 4)] + [("e01", 0, 1, dd, 4 + dd, 256) for dd in range(2, 4)]
-        units += [("e00", 0, 0, dd, 2 + dd, 256) for dd in range(4)]
-        for nm, hr, hc, dd, bank, c0 in units:
+            for q in range(8):
+                if q % 4 == 0:
+                    low(q // 4)
+                table(q, 6 + q % 2, TAB1[q])
+        units = [(nm, hr, hc, dd) for dd in range(4) for nm, hr, hc in (("e11", 1, 1), ("e01", 0, 1))]
+        units += [("e00", 0, 0, dd) for dd in range(4)]
+        banks = [2, 3, 4, 5] + ([6, 7] if last else [])
+        mm(P(1, 256, 512), A("s9"), A("zb"))
+        for u, (nm, hr, hc, dd) in enumerate(units):
+            bank, c0 = banks[u % len(banks)], 0
+            scalar = hr != hc or (nm, dd) in DIAG_ON_SCALAR
             for par in range(2):
                 p0 = 32 * dd
-                p1 = p0 + (32 if par else 16)
-                mm(P(bank, c0 + 128 * par, c0 + 128 * par + 128), A("zo" if par else "zb", 128 * hr, 128 * hr + 128, 1, p0, p1),
-                   A("zb", 128 * hc, 128 * hc + 128, 1, p0, p1))
+                p1 = p0 + (25 if par else 9)
+                o = P(bank, c0 + 128 * par, c0 + 128 * par + 128)
+                if scalar and hr == hc:
+                    mm(o, A("idb"), A("msk"), True, False)
+                mm(o, A("zo" if par else "zb", 128 * hr, 128 * hr + 128, 1, p0, p1),
+                   A("zb", 128 * hc, 128 * hc + 128, 1, p0, p1), not (scalar and hr == hc), True)
             for par in range(2):
                 d = 2 * dd + par
                 o = RAW(nm, T[nm][:, :, 16 * d:16 * d + 16], d, d + 1)
-                if hr == hc:
-                    tt(o, P(bank, c0 + 128 * par, c0 + 128 * par + 128), A("thr"), OP.is_ge)
-                else:
+                if scalar:
                     act(o, P(bank, c0 + 128 * par, c0 + 128 * par + 128), AF.Relu, bias=-8.0)
-            if (nm, dd) == ("e11", 0):
-                act(A("gbr"), IND(A("iom"), go), AF.Copy)
-        tt(A("nm"), IND(A("ne"), vo), A("diag"), OP.mult)
+                else:
+                    tt(o, P(bank, c0 + 128 * par, c0 + 128 * par + 128), A("thr"), OP.is_ge)
+        act(A("gbr"), IND(A("iom"), go), AF.Copy)
+        tt(A("nm"), P(1, 256, 512), A("diag"), OP.mult)
         scan(A("ns"), A("seg", 0, 256), A("nm"), 0.0, OP.mult, OP.add)
-        ts(A("zz", 160, 176), A("ns", 15, 256, 16), -1.0, OP.mult, 2.0 * K1, OP.add)
         mm(P(1, 64, 96), A("idf"), A("zz", 176, 208), True, False)
         for c in range(8):
             mm(P(1, 72 + c, 96, 16), RAW("e01", T.e01[:, c, :]), A("k1"), False, False)
@@ -432,47 +502,46 @@ def program(rank, T, topo):
         ts(col("sm", 3), col("sm", 2), 512.0, OP.is_ge, C["pm"], OP.mult)
         ts(vsu, col("sm", 3), col("sm", 2), OP.add)
         tt(A("zz", 112, 128), P(1, 80, 96), A("db", 48, 64), OP.min)
-        tt(A("zz", 80, 96), P(1, 64, 80), A("zz", 160, 176), OP.is_lt)
-        act(A("ax"), IND(A("zz", 80, 96), A("exu")), AF.Copy)
-        ts(A("zz", 64, 80), ri, -1.0 / 8, OP.mult, NV / 8.0, OP.add)
+        for s in range(2):
+            tt(A("ax", 128 * s, 128 * s + 128, 16), P(1, 64 + s, 80, 2), A("ns", 15 + 16 * s, 256, 32), OP.is_lt)
         ts(off, A("zz", 112, 128), float(NV), OP.add)
-        if not last:
-            table(0, 6, "a")
-            low(1)
         for s in range(2):
             mm(P(2, s, 256, 2), A("ax", 128 * s, 128 * s + 128), A("idb"))
         act(A("aw", 0, 256), P(2, 0, 256), AF.Copy)
-        act(A("am"), IND(A("aw"), pos), AF.Identity, scale=C["lt8"])
+        act(A("am"), IND(A("aw"), pos), AF.Identity, scale=float(NV))
         pick(P(2, 0, 16), "am", 0, 256)
-        tt(A("zz", 128, 144), P(2, 0, 16), A("zz", 64, 80), OP.mult)
-        if not last:
-            for q in range(1, 5):
-                table(q, 4 + (q + 2) % 4, "a")
+        tt(A("zz", 128, 144), P(2, 0, 16), A("zz", 64, 80), OP.max)
         tt(A("dlt"), IND(A("et"), off), A("gbr"), OP.mult)
-        tt(A("val"), IND(A("lw"), off), A("dlt"), OP.add)
-        tc(IND(A("lw"), off), A("val"))
-        act(P(3), A("lw", K1, K1 + V), AF.Copy)
+        tc(IND(A("dw"), off), A("dlt"))
+        if MERGE[t] == "v":
+            tt(P(3), A("dw", 0, V), A("dw", K1, K1 + V), OP.add)
+        else:
+            for h in range(2):
+                act(P(3 + h, 0, 256), A("dw", K1 + 256 * h, K1 + 256 * h + 256), AF.Copy)
+                tt(P(3 + h, 0, 256), P(3 + h, 0, 256), A("dw", 256 * h, 256 * h + 256), OP.add)
+        tc(IND(LWv, vsu), A("zz", 128, 144))
+        ends = [0] + ([] if MERGE[t] == "v" else [256]) + [512]
+        for v0, v1 in zip(ends, ends[1:]):
+            h = v0 // 256 if MERGE[t] == "a" else 0
+            tt(A("of" if last else "lw", v0, v1), A("lw", v0, v1), P(3 + h, v0 - 256 * h, v1 - 256 * h), OP.add)
         if not last:
-            for q in range(5, 7):
-                table(q, 4 + (q + 2) % 4, "a")
-        tt(A("zz", 144, 160), IND(LWv, vsu), A("zz", 128, 144), OP.add)
-        tc(IND(LWv, vsu), A("zz", 144, 160))
-        for v0, v1 in ([(0, 512)] if last else [(0, cuts[1][2]), (cuts[1][2], 512)]):
-            tt(A("lw", v0, v1), A("lw", v0, v1), P(3, v0, v1), OP.add)
-            tc(A("lu", v0, v1), A("lw", v0, v1))
-            if v1 < 512:
-                table(7, 5, "v")
+            m = PIECES[1][0][-1]
+            for h in range(2):
+                tc(A("lu", 256 * h + m, 256 * h + 256), A("lw", 256 * h + m, 256 * h + 256))
+            for h in range(2):
+                for b in range(2):
+                    mm(P(7, 256 * h, 256 * h + m), A("turn", 256 * h + 128 * b, 256 * h + 128 * b + 128),
+                       A("lw", 256 * b, 256 * b + m), b == 0, b == 1)
+                tc(A("lp", 256 * h, 256 * h + m), P(7, 256 * h, 256 * h + m))
         if not last:
-            iota(A("lw", K1, K1 + V), [[0, V]])
+            iota(A("dw", 0, SPARE), [[0, SPARE]])
             iota(A("ww", 0, 256), [[0, 256]])
 
-    exchange("lu", "dl", "rl", "bl", "a")
+    exchange("of", "dl", "rl", "bl", "a")
     landed("rx", "bx")
     dma("a", RAW("yx", T.yx[:]), RAW("rx", T.rx[:]))
     landed("rl", "bl")
-    dma("s", A("ou"), RAW("rl", T.rl[:]))
-    tc(A("of"), A("ou"))
-    dma("s", RAW("yl", T.yl[:]), A("of"))
+    dma("s", RAW("yl", T.yl[:]), RAW("rl", T.rl[:]))
     return ops
 
 
@@ -499,11 +568,12 @@ def width(x):
 def lasts(op, CYC=0.00095, GAT=1.56, SCA=3.8, PE=0.6, DMA=2.2, FAR=3.5):
     q, call, args, kw, nout, extra = op
     if call == "dma_start":
-        return 0.1, DMA
+        return 0.1, DMA + (0.5 if len(args) > 2 else 0.0)
     if call == "remote":
         return 1.0, 1.0
     if call == "landed":
-        return 0.0, FAR
+        link = {"ae": 0.3, "ax": 2.5, "al": 2.0}.get(args[1], 4.0)
+        return link, FAR - 2.0 + link
     n = width(args[0])
     aps = [x for x in args if isinstance(x, tuple) and x and x[0] in ("ap", "ind", "raw")]
     two = all(SCRATCH[x[1]][2] in (BF, U16) for x in aps if x[0] != "ind" and width(x) > 1)
@@ -516,7 +586,7 @@ def lasts(op, CYC=0.00095, GAT=1.56, SCA=3.8, PE=0.6, DMA=2.2, FAR=3.5):
     elif any(x[0] == "ind" for x in aps):
         c = 60 + GAT * n
     elif call == "tensor_tensor":
-        c = max(64, n if any(x[1].endswith("_") for x in aps) else 2 * n)
+        c = max(64, n if any(x[1].endswith("_") for x in aps[1:]) else 2 * n)
     else:
         c = max(64, n / 2 if two and q == "v" else n)
     return c * CYC, c * CYC
@@ -525,21 +595,110 @@ def lasts(op, CYC=0.00095, GAT=1.56, SCA=3.8, PE=0.6, DMA=2.2, FAR=3.5):
 def arrange(ops, deps):
     n = len(ops)
     dur = [lasts(o) for o in ops]
+    qs = [o[0] for o in ops]
+    reach, direct = [], []
+    for i in range(n):
+        r, keep = 0, []
+        for j in sorted(set(deps[i]), reverse=True):
+            if not r >> j & 1:
+                keep.append(j)
+                r |= reach[j] | 1 << j
+        reach.append(r)
+        direct.append(keep)
+    deps = direct
+    lag = lambda j, i: dur[j][0] if qs[j] == qs[i] == "p" else dur[j][1] + HOP
+    fore = [[(j, lag(j, i)) for j in set(deps[i])] for i in range(n)]
+    back = [[] for _ in ops]
+    for i in range(n):
+        for j, l in fore[i]:
+            back[j].append((i, dur[i][0] - dur[j][0] + l))
+
+    def fill(order, links, least):
+        start, busy = [0.0] * n, {q: [] for q in qs}
+        for i in order:
+            t, d, l = least[i], dur[i][0], busy[qs[i]]
+            for j, w in links[i]:
+                if start[j] + w > t:
+                    t = start[j] + w
+            lo, hi = 0, len(l)
+            while lo < hi:
+                m = (lo + hi) // 2
+                if l[m][1] <= t:
+                    lo = m + 1
+                else:
+                    hi = m
+            while lo < len(l) and t + d > l[lo][0]:
+                t = max(t, l[lo][1])
+                lo += 1
+            l.insert(lo, (t, t + d))
+            start[i] = t
+        return start
+
+    def ranked(key, links, span):
+        key = list(key)
+        for i in span:
+            for j, _ in links[i]:
+                if key[j] + 1e-6 > key[i]:
+                    key[i] = key[j] + 1e-6
+        return sorted(range(n), key=lambda i: key[i])
+
+    zero, tail = [0.0] * n, [d[1] - d[0] for d in dur]
     rest = [0.0] * n
     for i in range(n - 1, -1, -1):
-        rest[i] += dur[i][1] + HOP
-        for j in deps[i]:
-            rest[j] = max(rest[j], rest[i])
-    start, busy = [0.0] * n, {}
-    for i in sorted(range(n), key=lambda i: (-rest[i], i)):
-        t = max([start[j] + (dur[j][0] if ops[j][0] == ops[i][0] == "p" else dur[j][1] + HOP) for j in deps[i]] + [0.0])
-        for a, b in sorted(busy.get(ops[i][0], [])):
-            if t + dur[i][0] <= a:
-                break
-            t = max(t, b)
-        start[i] = t
-        busy.setdefault(ops[i][0], []).append((t, t + dur[i][0]))
-    return refine(ops, deps, sorted(range(n), key=lambda i: (start[i], -rest[i], i)))
+        rest[i] = max([rest[k] + lag(i, k) for k, _ in back[i]] + [dur[i][1]])
+    key, found, rnd = [-r for r in rest], [], 1
+    base, low = key, 1e9
+    for step in range(PASSES):
+        start = fill(ranked(key, fore, range(n)), fore, zero)
+        end = max(s + d[1] for s, d in zip(start, dur))
+        found.append((end, start))
+        late = fill(ranked([-s - d[0] for s, d in zip(start, dur)], back, range(n - 1, -1, -1)), back, tail)
+        key = [-r - d[0] for r, d in zip(late, dur)]
+        if end < low + SLACK:
+            base, low = key, min(low, end)
+        if step % 2 == 1:
+            rnd = (rnd * 1103515245 + 12345) % (1 << 31)
+            t0 = -low * ((rnd >> 8) % 1000) / 1000.0
+            key = []
+            for k in base:
+                if t0 < k < t0 + SPAN:
+                    rnd = (rnd * 1103515245 + 12345) % (1 << 31)
+                    k += SHAKE * ((rnd >> 8) % 1000 - 500) / 500.0
+                key.append(k)
+    cur, start = min(found, key=lambda f: f[0])
+    for step in range(MOVES):
+        order = sorted(range(n), key=lambda i: (start[i], i))
+        before, seen = {}, {}
+        for i in order:
+            before[i], seen[qs[i]] = seen.get(qs[i], -1), i
+        i, pairs = max(range(n), key=lambda i: start[i] + dur[i][1]), []
+        while start[i] > 1e-9:
+            js = [j for j, w in fore[i] if start[j] + w > start[i] - 1e-7]
+            if not js:
+                pairs.append((before[i], i))
+            i = js[0] if js else before[i]
+        rnd = (rnd * 1103515245 + 12345) % (1 << 31)
+        p, i = pairs[(rnd >> 8) % len(pairs)]
+        key = list(start)
+        far = 1e-4 + ((rnd >> 5) % 4) * 0.3
+        if (rnd >> 4) & 1:
+            key[p] = start[i] + far
+        else:
+            key[i] = start[p] - far
+            for k in range(i, -1, -1):
+                for j, _ in fore[k]:
+                    if key[j] > key[k] - 1e-6:
+                        key[j] = key[k] - 1e-6
+        new = fill(ranked(key, fore, range(n)), fore, zero)
+        if step % 4 == 0:
+            late = fill(ranked([-s - d[0] for s, d in zip(new, dur)], back, range(n - 1, -1, -1)), back, tail)
+            new = fill(ranked([-r - d[0] for r, d in zip(late, dur)], fore, range(n)), fore, zero)
+        end = max(s + d[1] for s, d in zip(new, dur))
+        if end <= cur + SLACK * (1.0 - step / MOVES) * ((rnd >> 12) % 100) / 100.0:
+            cur, start = end, new
+            found.append((end, new))
+    found.sort(key=lambda f: f[0])
+    return refine(ops, deps, [sorted(range(n), key=lambda i: (s[i], i)) for _, s in found[:TRIED]])
 
 
 def refine(ops, deps, first):
@@ -592,9 +751,8 @@ def refine(ops, deps, first):
         r = [run(seq, c) for c in range(len(cases))]
         return sum(x[0] / w for x, w in zip(r, WEIGHT)), [p for x in r for p in x[1]]
 
-    seq = {}
-    for i in first:
-        seq.setdefault(qs[i], []).append(i)
+    seqs = [{q: [i for i in f if qs[i] == q] for q in sorted(set(qs))} for f in first]
+    seq = min(seqs, key=lambda s: score(s)[0])
     cur, pairs = score(seq)
     best, keep, rnd = cur, {q: list(l) for q, l in seq.items()}, 12345
     for step in range(STEPS):
@@ -620,9 +778,10 @@ def refine(ops, deps, first):
     return sorted(range(n), key=lambda i: (ready[i], place[i]))
 
 
-CASES = [(0.00083, 1.3, 3.0, 0.6, 2.2, 4.0, 0.12), (0.00115, 1.9, 5.0, 0.5, 1.8, 2.5, 0.1)]
-WEIGHT = [85.0, 110.0]
-STEPS = 4000
+CASES = [(0.00083, 1.4, 3.3, 0.6, 2.2, 4.0, 0.12), (0.00112, 1.75, 4.5, 0.5, 2.0, 3.5, 0.12)]
+WEIGHT = [75.0, 95.0]
+STEPS, MOVES = 6000, 4000
+PASSES, TRIED, SHAKE, SLACK, SPAN = 3000, 40, 1.0, 0.2, 4.0
 HOP = 0.12
 ORDER = []
 
@@ -673,7 +832,7 @@ def rank_program(g, core, T, topo):
         touch.append((q, wr, rd, dma))
         deps.append(mine)
     if not ORDER:
-        gp = [i for i, o in enumerate(ops) if o[0] == "g"]
+        gp = [i for i, o in enumerate(ops) if o[1] == "remote"]
         after = dict(zip(gp[1:], gp))
         ORDER.extend(arrange(ops, [d + ([after[i]] if i in after and after[i] not in d else []) for i, d in enumerate(deps)]))
     order = ORDER
@@ -712,6 +871,12 @@ def rank_program(g, core, T, topo):
             continue
         a, k = [real(x) for x in args], {n: real(x) for n, x in kw.items()}
         e = queue[q]
+        if call == "dma_start" and len(args) > 2:
+            s = args[2]
+            e.dma_start(*a[:2]).then_inc(T.sem[s], 16)
+            count[s] = 16 * sum(1 for o in ops if o[1] == call and o[2][2:] == [s])
+            mark[i] = (s, count[s])
+            continue
         if call == "dma_start":
             s = "d%d" % ndma[0]
             ndma[0] += 1

from concourse.bass import DstId, RemoteDMATransfer
from concourse.mybir import AluOpType as OP, ActivationFunctionType as AF, AxisListType

N, V, B = 8, 512, 96
NV = N * V
K1 = 768
SPARE = K1 + V
WIN = SPARE + 256
SEG = 1024
F32, BF, I32, U16 = "float32", "bfloat16", "int32", "uint16"
MAGIC = 12582912.0


PIECES = [([0, 16, 48, 88, 136], [136, 196, 256], [392, 446, 490, 512], 446)] * 2
EMPTY, OWNERS, MERGE = "a", "vv", "aa"
TAB0, TAB1 = "aaavavav", "aaaaaaaa"
PREP = [0, 128, 256, 512]
DIAG_ON_SCALAR = [("e11", 1), ("e00", 3)]


def _sb(w, d):
    return ("sbuf", [128, w], d)


SCRATCH = {
    "se": ("dram", [8, 128, 4], I32), "sl": ("dram", [8, 128, 64], U16),
    "le": ("dram", [8, 128, 4], I32), "ll": ("dram", [8, 128, 64], U16),
    "dx": ("dram", [8, 128, 64], F32), "rx": ("dram", [8, 128, 64], F32),
    "dl": ("dram", [8, 128, 64], F32), "rl": ("dram", [8, 128, 64], F32),
    "xi": _sb(512, I32), "li": _sb(512, I32), "es": _sb(32, I32), "eu": _sb(32, I32),
    "xs": _sb(512, U16), "ls": _sb(512, U16), "xu": _sb(512, U16), "lu": _sb(512, U16),
    "of": _sb(512, F32),
    "tt": _sb(NV + 16, F32), "gg": _sb(8192, F32), "ms": _sb(8192, F32), "lw": _sb(528, F32),
    "hl": _sb(1024, BF), "a1": _sb(512, F32), "a2": _sb(512, F32), "xo": _sb(512, F32),
    "rep": _sb(512, BF), "jr": _sb(512, BF), "one": _sb(512, BF), "seg": _sb(SEG, BF), "j16": _sb(256, BF), "diag": _sb(256, BF),
    "iv": _sb(512, F32), "pi": _sb(4, I32), "pt": _sb(8, I32), "cc": _sb(40, F32),
    "tb": _sb(NV + 16, BF), "iom": _sb(NV, F32), "base": _sb(512, BF),
    "c2": _sb(16, F32), "nrow": _sb(528, F32), "bits": _sb(528, BF), "bito": _sb(528, BF),
    "bi": _sb(512, I32), "bj": _sb(512, I32), "bk": _sb(512, I32),
    "jg": _sb(128, BF), "bo": _sb(128, BF), "bof": _sb(128, F32), "idb": _sb(128, BF), "idf": _sb(128, F32),
    "nid": _sb(128, BF), "it": _sb(128, BF), "nit": _sb(128, BF), "tri": _sb(128, BF), "lt": _sb(128, BF),
    "sel": _sb(144, BF), "turn": _sb(512, F32), "j64": _sb(64, BF), "lp": _sb(512, U16), "jlo": _sb(128, BF), "jhi": _sb(128, BF),
    "gq": _sb(8, F32), "rw": _sb(16, BF), "kr": _sb(128, BF), "kt": _sb(128, BF), "thr": _sb(128, BF), "dth": _sb(96, F32),
    "db": _sb(64, F32), "k1": _sb(2, BF), "pw": _sb(64, F32), "c33": _sb(256, BF), "c32": _sb(16, BF), "q4": _sb(128, BF),
    "rep0": _sb(512, BF), "band": _sb(960, BF), "bitc": _sb(512, BF), "nb16": _sb(128, BF), "s10": _sb(128, BF), "s9": _sb(128, BF),
    "r910": _sb(128, BF), "msk": _sb(128, BF),
    "emp": _sb(512, BF), "et": _sb(WIN, BF), "dw": _sb(WIN, F32),
    "gt": _sb(512, BF), "sg": _sb(512, BF), "cum": _sb(512, BF), "junk": _sb(512, BF), "sm": _sb(16, F32),
    "us": _sb(128, U16), "ue": _sb(24, U16), "ed": _sb(96, F32), "edi": _sb(32, I32), "gb": _sb(96, F32), "df": _sb(96, F32),
    "p1": _sb(352, BF), "p2": _sb(352, BF), "cn": _sb(352, BF), "pr": _sb(352, BF), "ym": _sb(352, BF), "ys": _sb(352, BF),
    "zz": _sb(208, F32), "ze": _sb(48, F32), "ww": _sb(608, BF), "zb": _sb(256, BF), "zo": _sb(256, BF), "gbr": _sb(256, F32),
    "nm": _sb(256, BF), "ns": _sb(256, BF), "dlt": _sb(256, F32), "ax": _sb(256, BF), "aw": _sb(512, BF),
    "am": _sb(256, BF),
    "e00": ("sbuf", [128, 8, 128], BF), "e01": ("sbuf", [128, 8, 128], BF), "e11": ("sbuf", [128, 8, 128], BF),
}
for _k in range(8):
    SCRATCH["p%d_" % _k] = ("psum", [128, 512], F32)
NDMA = 24
SEMAPHORES = ["sv", "sa", "sp", "sg", "ae", "ax", "al", "bx", "bl", "out", "in"] + ["d%d" % k for k in range(NDMA)]


def program(rank, T, topo):
    ops = []

    def A(name, c0=0, c1=None, step=1, p0=0, p1=128):
        if c1 is None:
            c1 = SCRATCH[name][1][1]
        return ("ap", name, c0, c1, step, p0, p1)

    def col(name, c):
        return A(name, c, c + 1)

    def P(k, c0=0, c1=512, step=1, p0=0, p1=128):
        return A("p%d_" % k, c0, c1, step, p0, p1)

    def IND(win, off):
        return ("ind", win, off)

    def RAW(name, ap, c0=0, c1=1 << 20):
        return ("raw", name, ap, c0, c1)

    def put(q, call, args, kw=None, nout=1, extra_out=()):
        ops.append((q, call, args, kw or {}, nout, extra_out))

    def tc(out, in_): put("v", "tensor_copy", [out, in_])
    def tt(out, a, b, op): put("v", "tensor_tensor", [out, a, b, op])
    def ts(out, a, s1, op0, s2=None, op1=None):
        put("v", "tensor_scalar", [out, a, s1, s2, op0] + ([op1] if op1 is not None else []))
    def scan(out, d0, d1, init, op0, op1): put("v", "tensor_tensor_scan", [out, d0, d1, init, op0, op1])
    def ms(out, c): put("v", "memset", [out, c])
    def act(out, in_, f, bias=None, scale=None, acc=None):
        kw = {}
        if bias is not None: kw["bias"] = bias
        if scale is not None: kw["scale"] = scale
        if acc is not None: kw["accum_out"] = acc
        put("a", "activation", [out, in_, f], kw, 1, (acc,) if acc is not None else ())
    def lin(out, in_, scale=None, bias=None): act(out, in_, AF.Identity, bias, scale)
    def mm(out, l, r, st=True, sp=True): put("p", "matmul", [out, l, r, st, sp])
    def iota(out, pat, base=0, cm=0):
        put("g", "iota", [out, pat, base, cm], {} if SCRATCH[out[1]][2] == I32 else {"allow_small_or_imprecise_dtypes": True})
    def dma(q, out, in_, shared=None): put(q, "dma_start", [out, in_] + ([shared] if shared else []))

    me = T.cores[rank]
    own = dict(p0=16 * rank, p1=16 * rank + 16)

    def exchange(buf, src, dst, sem, q2="s"):
        dma("s", RAW(src, T[src][:]), A(buf))
        dma(q2, RAW(dst, T[dst][rank]), A(buf, **own))
        send(src, lambda r: T[src][r], T[dst][rank], sem)

    def send(src, piece, slot, sem):
        far = [r for r in range(N) if r != rank and topo.chip(T.cores[r]) != topo.chip(me)]
        used, tr, total = set(), [], 0
        for r in far + [r for r in range(N) if r != rank and r not in far]:
            free = [e for e in topo.engines(me, T.cores[r]) if e not in used]
            take = free[:1] if r in far else free[-1:]
            used.update(take)
            rid, pid, _ = topo.addr(T.cores[r])
            tr.append(RemoteDMATransfer(dst_ids=[DstId(rid=rid, pnc=pid)], dma_engine_mask=sum(1 << e for e in take),
                                        remote_sem=T.sem[sem], src=piece(r), dst=slot))
            total += len(take)
        ops.append(("g", "remote", [RAW(src, None), tr, total, sem], {}, 0, ()))

    def landed(dst, sem):
        ops.append(("x", "landed", [RAW(dst, None), sem, N - 1], {}, 1, ()))

    C = {k: col("cc", i) for i, k in enumerate(
        ["pm", "pg", "od", "p32", "p64", "pf", "g512", "b2", "b3", "key", "cb", "ic", "le8", "pw", "x1", "x2", "x3", "x4",
         "m1", "m2", "m3", "p64h", "lo", "hi", "t16", "x0", "g15", "d9", "ma", "mb", "d13", "y1", "y2"])}
    D = lambda k: col("diag", k)

    ms(A("es", 24, 32), 0)
    dma("a", A("li"), RAW("l0", T.l0[:]))
    for r in range(N):
        for h in range(2):
            dma("sa"[h], A("xi", 64 * r, 64 * r + 64, 1, 64 * h, 64 * h + 64),
                RAW("x0", T.x0[16 * r:16 * r + 16, 256 * h:256 * h + 256]), "in")
    dma("a", A("es", 0, 12), RAW("ea", T.ea[:]))
    dma("s", A("es", 12, 24), RAW("eb", T.eb[:]))
    dma("a", A("es", 24, 26), RAW("u", T.u[:]))
    iota(col("pi", 0), [[0, 1]], 0, 1)
    iota(A("j16"), [[0, 16], [1, 16]])
    iota(A("iv"), [[1, 512]])
    tc(A("ls"), A("li"))
    tc(A("xs"), A("xi"))
    tc(RAW("xu", T.xu[:, 64 * rank:64 * rank + 64]), RAW("xs", T.xs[:, 64 * rank:64 * rank + 64]))
    send("xs", lambda r: T.xs[:, 64 * r:64 * r + 64], T.xu[:, 64 * rank:64 * rank + 64], "ax")
    exchange("ls", "sl", "ll", "al")
    exchange("es", "se", "le", "ae", "a")
    ms(A("pw", 0, 16), 0.5)
    ms(A("pw", 16, 32), 0.0)
    ts(col("pt", 0), col("pi", 0), 15, OP.bitwise_and)
    ts(col("pt", 1), col("pi", 0), 4, OP.arith_shift_right)
    ts(col("pt", 2), col("pi", 0), 4, OP.arith_shift_right, 1, OP.bitwise_and)
    ts(col("pt", 3), col("pi", 0), 96, OP.bitwise_and)
    ts(col("pt", 4), col("pi", 0), 63, OP.bitwise_and)
    scan(A("pw", 32, 48), A("pw", 0, 16), A("pw", 16, 32), 2.0, OP.mult, OP.add)
    tc(C["pf"], col("pi", 0))
    tc(A("cc", 0, 5), A("pt", 0, 5))
    ms(A("pw", 41, 45), 1.0)
    ms(A("one"), 1.0)
    ms(A("pw", 41, 45, 2), 1.0 / 64)
    ts(A("diag"), A("j16"), C["pm"], OP.is_equal)
    lin(C["g512"], C["pg"], 512.0)
    tt(A("pw", 48, 64), A("pw", 32, 48), A("diag", 0, 16), OP.mult)
    put("v", "tensor_reduce", [C["pw"], A("pw", 48, 64), AxisListType.X, OP.add])
    lin(C["x0"], D(9), 1.0, D(10))
    lin(C["m3"], D(11), 1.0, D(12))
    lin(C["m1"], C["x0"], 1.0 / 64, C["m3"])
    lin(C["m2"], D(9), -1.0)
    lin(C["mb"], C["m3"], 1.0, D(13))
    lin(C["ma"], C["mb"], -1.0, 1.0)
    lin(C["d13"], D(13))
    lin(A("c2", 8, 16), A("j16", 0, 8), C["d13"])
    tt(A("c2", 0, 8), A("c2", 8, 16), A("diag", 0, 8), OP.add)
    act(A("a1"), A("iv"), AF.Identity, bias=-0.499, scale=C["pw"])
    iota(A("jr"), [[16, 4], [0, 8], [1, 16]])
    iota(A("rep0"), [[1, 4], [0, 8], [4, 16]])
    iota(A("band"), [[1, 4], [4, 240]], -448)
    iota(A("jg"), [[1, 8], [0, 16]])
    iota(A("kr"), [[32, 4], [1, 2], [2, 16]])
    iota(A("ww"), [[0, 608]])
    iota(A("j64"), [[16, 8], [1, 8]])
    iota(A("turn"), [[0, 512]])
    iota(A("lw", 512, 528), [[0, 16]], NV)
    iota(A("c33"), [[0, 256]], 33)
    iota(A("dw"), [[0, WIN]])
    iota(A("et"), [[0, WIN]])
    iota(A("aw"), [[0, 512]])
    iota(A("ax"), [[0, 256]])
    iota(A("iom"), [[1, NV]], -NV)

    tc(A("bi"), A("a1"))
    ms(A("seg"), 1.0)
    ts(A("bk"), A("bi"), 63, OP.bitwise_and)
    ts(A("bj"), A("bi"), 1, OP.bitwise_and)
    ts(A("base"), A("bk"), C["m1"], OP.mult, C["m2"], OP.add)
    for q in range(N):
        act(A("tb", q * V, q * V + V), A("base"), AF.Identity, bias=col("c2", q))
    ms(A("seg", 0, SEG, 16), 0.0)
    ms(A("k1", 0, 1), 1.0)
    ms(A("k1", 1, 2), float(K1))
    ms(A("c32"), 32.0)
    ms(A("q4"), -1.0 / 256)
    ms(A("zz", 176, 192), 0.0)
    ms(A("tt", NV, NV + 16), 0.0)
    ms(A("nrow", 512, 528), 0.0)
    ms(A("bits", 512, 528), 0.0)
    ms(A("bito", 512, 528), 0.0)
    lin(C["y1"], D(9), 64.0, D(10))
    lin(C["x1"], C["y1"], 64.0)
    lin(C["y2"], D(11), 64.0, D(12))
    lin(C["x2"], D(13), 512.0, C["y2"])
    act(C["le8"], C["pm"], AF.Sign, bias=8.5, scale=-1.0)
    lin(C["b2"], C["le8"], 1.0, 1.0)
    lin(C["b3"], C["b2"], -0.5)
    lin(C["le8"], C["b2"], 0.5)
    lin(C["cb"], C["pm"], 2.0, 1.0)
    ts(C["ic"], C["pm"], 8.0, OP.is_ge, 33.0, OP.mult)
    lin(C["lo"], D(10), 4.0, C["b3"])
    lin(C["x3"], D(10), 15.0, C["le8"])
    lin(C["hi"], D(9), 2.0, C["x3"])
    lin(C["t16"], D(10), 16.0)
    lin(C["x4"], C["pm"], 2.0, C["od"])
    lin(C["p64h"], C["p64"], 1.0, 64.0)
    ts(A("gq"), A("j16", 0, 8), C["pg"], OP.is_equal)
    lin(A("db", 0, 16), A("j16", 0, 16), 16.0, C["pm"])
    lin(A("dth"), A("diag", 0, 96), 1.0e7, -1.0e7)
    lin(C["key"], C["x4"], 1.0, C["p32"])
    lin(A("rw", 0, 8), A("gq"), C["x1"])
    lin(A("rw", 8, 16), A("gq"), C["x2"])
    lin(A("db", 16, 32), A("db", 0, 16), 1.0, 256.0 - 31)
    lin(A("db", 32, 48), A("db", 0, 16), 1.0, 512.0 - 31)
    lin(A("db", 48, 64), A("db", 0, 16), 1.0, float(SPARE - NV))
    lin(A("tb", NV, NV + 16), A("one", 0, 16), 0.0, D(8))
    ts(A("idb"), A("iv", 0, 128), C["pf"], OP.is_equal)
    lin(A("nid"), A("idb"), -1.0)
    lin(A("idf"), A("idb"))
    ts(A("jlo"), A("iv", 0, 128), C["p64"], OP.is_equal)
    ts(A("jhi"), A("iv", 0, 128), C["p64h"], OP.is_equal)
    ts(A("bitc"), A("bj"), C["b2"], OP.mult, C["b3"], OP.add)
    lin(A("nrow", 0, 512), A("iv"), 1.0, C["g512"])
    lin(A("bito", 0, 512), A("bitc"), C["od"])
    ts(A("bo"), A("jg"), C["pg"], OP.is_equal)
    lin(A("bof"), A("bo"))
    lin(A("nb16"), A("bo"), -16.0)
    lin(A("s10"), A("bo"), C["t16"])
    lin(C["d9"], D(9))
    lin(A("s9"), A("bo"), C["d9"])
    ts(A("r910"), A("j16", 0, 128), 9.0, OP.is_ge)
    ts(A("lt"), A("j16", 0, 128), 10.0, OP.is_le)
    tt(A("kt"), A("r910"), A("lt"), OP.mult)
    ts(A("rep"), A("jr"), C["p64"], OP.is_equal)
    ts(A("rep0"), A("rep0"), C["p64"], OP.is_equal)
    ts(A("band"), A("band"), C["p64"], OP.is_equal)
    for h in range(2):
        for b in range(2):
            ts(A("turn", 256 * h + 128 * b + b, 256 * h + 128 * b + 128, 2), A("j64"), 8.0 * h, OP.add, C["pf"], OP.is_equal)
    lin(C["g15"], C["pg"], 16.0, 15.0)
    ts(A("sel"), A("iv", 0, 144), C["g15"], OP.is_equal, C["le8"], OP.mult)
    tt(A("r910"), A("kt"), A("bo"), OP.mult)
    ts(A("lt"), A("iv", 0, 128), C["pf"], OP.is_gt)
    tt(A("tri"), A("lt"), A("bo"), OP.mult)
    ts(A("msk"), A("kr"), C["key"], OP.is_le, -16.0, OP.mult)
    tt(A("it"), A("idb"), A("tri"), OP.subtract)
    lin(A("nit"), A("it"), -1.0)
    lin(A("thr"), A("msk"), -1.0, 9.0)

    landed("xu", "ax")
    landed("le", "ae")
    dma("s", A("eu"), RAW("le", T.le[:]))
    landed("ll", "al")
    dma("s", A("lu"), RAW("ll", T.ll[:]))
    for h in range(2):
        dma("as"[h], A("lp", 256 * h, 256 * h + 256), RAW("ll", T.ll[:, 64 * h:64 * h + 64, :]))
    ts(A("ed", 0, 12), A("eu", 0, 12), C["g512"], OP.add)
    tc(A("ed", 12, 24), A("eu", 12, 24))
    ts(A("sm", 10, 12), A("eu", 24, 26), -1.0, OP.mult, 65535.0, OP.add)
    tc(A("ue"), A("ed", 0, 24))
    tt(A("ed", 24, 36), A("ed", 0, 12), A("ed", 12, 24), OP.subtract)

    HL = lambda h, up: A("hl", 512 * h, 512 * h + 512, 1, 64 * up, 64 * up + 64)

    def low(h):
        tt(HL(h, 1 - h), P(0, p0=64 * h, p1=64 * h + 64), HL(h, h), OP.subtract)

    def table(q, bank, eng):
        mm(P(bank), A("rep", 128 * (q % 4), 128 * (q % 4) + 128), A("hl", 512 * (q // 4), 512 * (q // 4) + 512))
        if eng == "a":
            act(A("tt", q * V, q * V + V), P(bank), AF.Copy)
        else:
            tc(A("tt", q * V, q * V + V), P(bank))

    landing = [(q, h, k) for q in range(N) for h in range(2) for k in range(4)]
    came = lambda q, h: A("hl", 512 * h + 64 * q, 512 * h + 64 * q + 64)
    for c0, c1 in zip(PREP, PREP[1:]):
        part = lambda h, up: A("hl", 512 * h + c0, 512 * h + c1, 1, 64 * up, 64 * up + 64)
        tc(P(1, c0, c1), A("xu", c0, c1))
        for h in range(2):
            ts(part(h, h), A("xu", c0, c1, 1, 64 * h, 64 * h + 64), 1.0, OP.mult)
            tt(part(h, 1 - h), P(1, c0, c1, 1, 64 * h, 64 * h + 64), part(h, h), OP.subtract)
    for q, h, k in landing:
        bank = 2 + q % 6
        mm(P(bank, 256 * h + 64 * k, 256 * h + 64 * k + 64), A("rep0", 128 * k, 128 * k + 128), came(q, h))
        if (h, k) == (1, 3):
            if TAB0[q] == "a":
                act(A("tt", q * V, q * V + V), P(bank), AF.Copy)
            else:
                tc(A("tt", q * V, q * V + V), P(bank))

    def own_values(bank, close):
        for q, h, k in landing:
            c = 240 * k + 112 - 16 * q
            mm(P(bank, 256 * h + 64 * k, 256 * h + 64 * k + 64), A("band", c, c + 128), came(q, h), False, close and (q, h, k) == landing[-1])

    mm(P(0), A("ax", 0, 128), A("one"), True, False)
    own_values(0, True)

    TW, TBW = A("tt"), A("tb")

    def pick(out, name, j0, n, first=True):
        for r in range(16):
            mm(out, A("sel", 15 - r, 143 - r), A(name, j0 + r, j0 + n, 16), first and r == 0, r == 15)

    def place(j0, n, rec, giv, own32, init, dump, pos, between=lambda: None):
        k = n // 16
        r = lambda name: A(name, j0, j0 + n)
        if j0 or OWNERS[t] == "a":
            lin(r("p1"), IND(TBW, rec), C["ma"])
        else:
            ts(r("p1"), IND(TBW, rec), C["ma"], OP.mult)
        lin(r("p2"), IND(TBW, giv), C["mb"])
        scan(r("cn"), r("p1"), A("c33", 0, n), init, OP.add, OP.min)
        scan(r("pr"), r("cn"), r("p1"), 0.0, OP.max, OP.mult)
        y = P(6 if j0 else 1, 0, k)
        mm(y, A("nid"), A("c32", 0, k), True, False)
        pick(y, "pr", j0, n, False)
        between()
        z = lambda c: A("ze" if j0 else "zz", c, c + k)
        tt(z(0), y, dump, OP.mult)
        tt(z(16), y, own32, OP.add)
        tt(z(32), z(0), z(16), OP.max)
        ts(pos, z(32), 31.0, OP.add)
        tt(IND(A("ww"), pos), r("p1"), r("p2"), OP.add)

    def edges(t):
        c = 6 * t
        act(A("gb"), IND(TW, A("ue", 12 + c, 18 + c)), AF.Copy)
        tt(A("df"), IND(TW, A("ue", c, c + 6)), A("gb"), OP.subtract)
        mm(P(6, 0, B), A("bof"), A("df"))
        yield
        tt(A("ym", 256, 352), P(6, 0, B), A("dth"), OP.is_le)
        scan(A("ys", 256, 352), A("seg", 0, B), A("ym", 256, 352), 0.0, OP.mult, OP.add)
        tt(A("ed", 48, 54), A("ys", 256 + 15, 352, 16), A("ed", 24 + c, 30 + c), OP.mult)
        tt(A("edi", 0, 6), A("ed", 48, 54), A("ed", 12 + c, 18 + c), OP.add)
        tt(A("ed", 64, 70), A("ed", c, 6 + c), A("ed", 48, 54), OP.subtract)
        tc(A("us", 12, 18), A("edi", 0, 6))
        tc(A("us", 18, 24), A("ed", 64, 70))
        ts(A("edi", 8, 14), A("edi", 0, 6), 4, OP.arith_shift_right, 0xE0, OP.bitwise_and)
        yield
        place(256, B, A("us", 12, 18), A("us", 18, 24), A("edi", 8, 14), C["ic"], A("db", 32, 38), A("us", 24, 30))

    def gather(eng, v0, v1):
        o, i = A("gg", 16 * v0, 16 * v1), IND(TW, A("lu", v0, v1))
        if eng == "a":
            act(o, i, AF.Copy)
        else:
            tc(o, i)

    def top(v0, v1):
        scan(A("ms", 16 * v0, 16 * v1), A("seg", 0, 16 * (v1 - v0)), A("gg", 16 * v0, 16 * v1), 0.0, OP.mult, OP.max)

    def paired(c0, c1):
        a, b = A("gg", 16 * c0, 16 * c1), A("gg", 4096 + 16 * c0, 4096 + 16 * c1)
        act(a, IND(TW, A("lp", c0, c1)), AF.Copy)
        tt(b, IND(TW, A("lp", 256 + c0, 256 + c1)), a, OP.max)
        for h in range(2):
            scan(A("ms", 4096 * h + 16 * c0 + 1, 4096 * h + 16 * c1, 2), A("seg", 0, 16 * (c1 - c0), 2),
                 A("gg", 4096 + 16 * c0 + h, 4096 + 16 * c1, 2), 0.0, OP.mult, OP.max)

    def M(v0, v1):
        return A("ms", 16 * v0 + 15, 16 * v1, 16)

    def ripe(v0, v1, part):
        if part == 0:
            tt(A("gt", v0, v1), P(0, v0, v1), M(v0, v1), OP.is_gt)
            mm(P(2, v0, v1), A("s10"), A("bits", v0, v1), True, False)
            mm(P(2, v0, v1), A("nb16"), A("emp", v0, v1), False, False)
            mm(P(2, v0, v1), A("bo"), A("gt", v0, v1), False, True)
            mm(P(4, v0, v1), A("idf"), M(v0, v1), False, v1 == V)
        elif part == 1:
            act(A("sg", v0, v1), P(2, v0, v1), AF.Sign, bias=-11.5)
        elif part == 2:
            scan(A("cum", v0, v1), A("sg", v0, v1), A("one", 0, v1 - v0), 0.0 if v0 == 0 else col("cum", v0 - 1), OP.add, OP.add)
        else:
            act(A("junk", v0, v1), A("cum", v0, v1), AF.Sign, bias=C["cb"], scale=-1.0, acc=col("sm", 0 if v0 == 0 else 4))

    for t in range(2):
        last = t == 1
        pairs, low_, high, RA = PIECES[t]
        for _ in edges(t):
            pass
        if t == 0:
            tc(A("lw", 0, 512), A("lu"))
            ts(A("emp"), A("lu"), float(NV), OP.is_equal)
        elif EMPTY == "v":
            ts(A("emp"), A("lw", 0, 512), float(NV), OP.is_equal)
        else:
            act(A("emp"), A("lw", 0, 512), AF.Relu, bias=1.0 - NV)
        mm(P(5), A("idb"), A("bitc"), True, False)
        mm(P(5), A("r910"), A("emp"), False, True)
        ts(A("bits", 0, 512), P(5), C["lo"], OP.max, C["hi"], OP.min)
        mm(P(3), A("it"), A("emp"))
        mm(P(4), A("q4"), A("one"), True, False)
        if t == 0:
            own_values(4, False)
        else:
            mm(P(4), A("jlo"), A("hl", 0, V), False, False)
            mm(P(4), A("jhi"), A("hl", V, 2 * V), False, False)
        for c0, c1 in zip(pairs, pairs[1:]):
            paired(c0, c1)
        for v0, v1 in list(zip(low_, low_[1:])) + list(zip(high, high[1:])):
            gather("a", v0, v1)
            top(v0, v1)
        for k in range(4):
            ripe(0, RA, k)
        ripe(RA, 512, 0)
        ts(col("sm", 1), col("sm", 0), 0.5, OP.mult, 256.0, OP.add)
        act(A("et", 0, 512), P(3), AF.Relu)
        for k in (1, 2, 3):
            ripe(RA, 512, k)
        vs, vsu = A("us", 32, 33), A("us", 34, 35)
        ts(vs, col("sm", 4), 0.5, OP.mult, col("sm", 1), OP.add)
        act(A("a2"), P(4), AF.Relu, bias=col("sm", 10 + t), scale=-0.5)
        act(A("a1"), A("a2"), AF.Identity, bias=MAGIC + 65535.0, scale=-1.0)
        mm(P(3), A("it"), A("emp"), True, False)
        mm(P(3), A("nit"), A("et", 0, 512), False, True)
        LWv = A("lw", 0, 528)
        ri, gi, pos = A("us", 48, 64), A("us", 64, 80), A("us", 80, 96)
        tc(ri, IND(LWv, vs))
        tc(gi, IND(A("nrow"), vs))

        def between():
            tc(A("edi", 16, 32), ri)
            ts(col("sm", 2), col("sm", 4), 0.5, OP.mult, col("sm", 1), OP.add)
            ts(A("edi", 16, 32), A("edi", 16, 32), 4, OP.arith_shift_right, 0xE0, OP.bitwise_and)
            tc(A("zz", 64, 80), ri)
            if last:
                act(A("xo"), A("a1"), AF.Relu, bias=-MAGIC)
                exchange("xo", "dx", "rx", "bx")
            else:
                act(P(0), A("a1"), AF.Relu, bias=-MAGIC)
                for h in range(2):
                    act(HL(h, h), A("a1", p0=64 * h, p1=64 * h + 64), AF.Relu, bias=-MAGIC)
            act(A("et", K1, K1 + V), P(3), AF.Relu)

        place(0, 256, ri, gi, A("edi", 16, 32), col("cn", 351), A("db", 16, 32), pos, between)
        for s in range(2):
            mm(P(1, s, 32, 2), A("ww", s, 256, 2), A("rw"))
        vo, go, off = A("us", 96, 112), A("us", 112, 128), A("us", 64, 80)
        ts(vo, P(1, 0, 16), float(NV), OP.add, 512.0, OP.min)
        tc(go, P(1, 16, 32))
        tc(A("zb"), IND(A("bits"), vo))
        act(A("zo"), IND(A("bito"), vo), AF.Copy)
        tc(A("zz", 192, 208), P(1, 0, 16))
        if not last:
            for q in range(8):
                if q % 4 == 0:
                    low(q // 4)
                table(q, 6 + q % 2, TAB1[q])
        units = [(nm, hr, hc, dd) for dd in range(4) for nm, hr, hc in (("e11", 1, 1), ("e01", 0, 1))]
        units += [("e00", 0, 0, dd) for dd in range(4)]
        banks = [2, 3, 4, 5] + ([6, 7] if last else [])
        mm(P(1, 256, 512), A("s9"), A("zb"))
        for u, (nm, hr, hc, dd) in enumerate(units):
            bank, c0 = banks[u % len(banks)], 0
            scalar = hr != hc or (nm, dd) in DIAG_ON_SCALAR
            for par in range(2):
                p0 = 32 * dd
                p1 = p0 + (25 if par else 9)
                o = P(bank, c0 + 128 * par, c0 + 128 * par + 128)
                if scalar and hr == hc:
                    mm(o, A("idb"), A("msk"), True, False)
                mm(o, A("zo" if par else "zb", 128 * hr, 128 * hr + 128, 1, p0, p1),
                   A("zb", 128 * hc, 128 * hc + 128, 1, p0, p1), not (scalar and hr == hc), True)
            for par in range(2):
                d = 2 * dd + par
                o = RAW(nm, T[nm][:, :, 16 * d:16 * d + 16], d, d + 1)
                if scalar:
                    act(o, P(bank, c0 + 128 * par, c0 + 128 * par + 128), AF.Relu, bias=-8.0)
                else:
                    tt(o, P(bank, c0 + 128 * par, c0 + 128 * par + 128), A("thr"), OP.is_ge)
        act(A("gbr"), IND(A("iom"), go), AF.Copy)
        tt(A("nm"), P(1, 256, 512), A("diag"), OP.mult)
        scan(A("ns"), A("seg", 0, 256), A("nm"), 0.0, OP.mult, OP.add)
        mm(P(1, 64, 96), A("idf"), A("zz", 176, 208), True, False)
        for c in range(8):
            mm(P(1, 72 + c, 96, 16), RAW("e01", T.e01[:, c, :]), A("k1"), False, False)
            mm(P(1, 72 + c, 96, 16), RAW("e11", T.e11[:, c, :]), A("k1"), False, False)
        for c in range(8):
            mm(P(1, 64 + c, 96, 16), RAW("e00", T.e00[:, c, :]), A("k1"), False, c == 7)
        ts(col("sm", 3), col("sm", 2), 512.0, OP.is_ge, C["pm"], OP.mult)
        ts(vsu, col("sm", 3), col("sm", 2), OP.add)
        tt(A("zz", 112, 128), P(1, 80, 96), A("db", 48, 64), OP.min)
        for s in range(2):
            tt(A("ax", 128 * s, 128 * s + 128, 16), P(1, 64 + s, 80, 2), A("ns", 15 + 16 * s, 256, 32), OP.is_lt)
        ts(off, A("zz", 112, 128), float(NV), OP.add)
        for s in range(2):
            mm(P(2, s, 256, 2), A("ax", 128 * s, 128 * s + 128), A("idb"))
        act(A("aw", 0, 256), P(2, 0, 256), AF.Copy)
        act(A("am"), IND(A("aw"), pos), AF.Identity, scale=float(NV))
        pick(P(2, 0, 16), "am", 0, 256)
        tt(A("zz", 128, 144), P(2, 0, 16), A("zz", 64, 80), OP.max)
        tt(A("dlt"), IND(A("et"), off), A("gbr"), OP.mult)
        tc(IND(A("dw"), off), A("dlt"))
        if MERGE[t] == "v":
            tt(P(3), A("dw", 0, V), A("dw", K1, K1 + V), OP.add)
        else:
            for h in range(2):
                act(P(3 + h, 0, 256), A("dw", K1 + 256 * h, K1 + 256 * h + 256), AF.Copy)
                tt(P(3 + h, 0, 256), P(3 + h, 0, 256), A("dw", 256 * h, 256 * h + 256), OP.add)
        tc(IND(LWv, vsu), A("zz", 128, 144))
        ends = [0] + ([] if MERGE[t] == "v" else [256]) + [512]
        for v0, v1 in zip(ends, ends[1:]):
            h = v0 // 256 if MERGE[t] == "a" else 0
            tt(A("of" if last else "lw", v0, v1), A("lw", v0, v1), P(3 + h, v0 - 256 * h, v1 - 256 * h), OP.add)
        if not last:
            m = PIECES[1][0][-1]
            for h in range(2):
                tc(A("lu", 256 * h + m, 256 * h + 256), A("lw", 256 * h + m, 256 * h + 256))
            for h in range(2):
                for b in range(2):
                    mm(P(7, 256 * h, 256 * h + m), A("turn", 256 * h + 128 * b, 256 * h + 128 * b + 128),
                       A("lw", 256 * b, 256 * b + m), b == 0, b == 1)
                tc(A("lp", 256 * h, 256 * h + m), P(7, 256 * h, 256 * h + m))
        if not last:
            iota(A("dw", 0, SPARE), [[0, SPARE]])
            iota(A("ww", 0, 256), [[0, 256]])

    exchange("of", "dl", "rl", "bl", "a")
    landed("rx", "bx")
    dma("a", RAW("yx", T.yx[:]), RAW("rx", T.rx[:]))
    landed("rl", "bl")
    dma("s", RAW("yl", T.yl[:]), RAW("rl", T.rl[:]))
    return ops


def spans(x):
    if not isinstance(x, tuple) or not x or x[0] not in ("ap", "ind", "raw"):
        return []
    if x[0] == "ind":
        return spans(x[1]) + spans(x[2])
    if x[0] == "raw":
        return [(x[1], x[3], x[4])]
    if x[1].endswith("_"):
        return [(x[1], 0, 1 << 20)]
    return [(x[1], x[2], x[3])]


def width(x):
    if x[0] == "ind":
        return 16 * width(x[2])
    if x[0] == "raw":
        return 128
    return (x[3] - x[2] + x[4] - 1) // x[4]


def lasts(op, CYC=0.00095, GAT=1.56, SCA=3.8, PE=0.6, DMA=2.2, FAR=3.5):
    q, call, args, kw, nout, extra = op
    if call == "dma_start":
        return 0.1, DMA + (0.5 if len(args) > 2 else 0.0)
    if call == "remote":
        return 1.0, 1.0
    if call == "landed":
        link = {"ae": 0.3, "ax": 2.5, "al": 2.0}.get(args[1], 4.0)
        return link, FAR - 2.0 + link
    n = width(args[0])
    aps = [x for x in args if isinstance(x, tuple) and x and x[0] in ("ap", "ind", "raw")]
    two = all(SCRATCH[x[1]][2] in (BF, U16) for x in aps if x[0] != "ind" and width(x) > 1)
    if call == "matmul":
        c = PE * max(64, n) * (4 if SCRATCH[args[1][1]][2] == F32 else 1)
    elif call == "iota":
        c = 160 + 2 * n
    elif args[0][0] == "ind":
        c = 60 + SCA * n
    elif any(x[0] == "ind" for x in aps):
        c = 60 + GAT * n
    elif call == "tensor_tensor":
        c = max(64, n if any(x[1].endswith("_") for x in aps[1:]) else 2 * n)
    else:
        c = max(64, n / 2 if two and q == "v" else n)
    return c * CYC, c * CYC


def arrange(ops, deps):
    n = len(ops)
    dur = [lasts(o) for o in ops]
    qs = [o[0] for o in ops]
    reach, direct = [], []
    for i in range(n):
        r, keep = 0, []
        for j in sorted(set(deps[i]), reverse=True):
            if not r >> j & 1:
                keep.append(j)
                r |= reach[j] | 1 << j
        reach.append(r)
        direct.append(keep)
    deps = direct
    lag = lambda j, i: dur[j][0] if qs[j] == qs[i] == "p" else dur[j][1] + HOP
    fore = [[(j, lag(j, i)) for j in set(deps[i])] for i in range(n)]
    back = [[] for _ in ops]
    for i in range(n):
        for j, l in fore[i]:
            back[j].append((i, dur[i][0] - dur[j][0] + l))

    def fill(order, links, least):
        start, busy = [0.0] * n, {q: [] for q in qs}
        for i in order:
            t, d, l = least[i], dur[i][0], busy[qs[i]]
            for j, w in links[i]:
                if start[j] + w > t:
                    t = start[j] + w
            lo, hi = 0, len(l)
            while lo < hi:
                m = (lo + hi) // 2
                if l[m][1] <= t:
                    lo = m + 1
                else:
                    hi = m
            while lo < len(l) and t + d > l[lo][0]:
                t = max(t, l[lo][1])
                lo += 1
            l.insert(lo, (t, t + d))
            start[i] = t
        return start

    def ranked(key, links, span):
        key = list(key)
        for i in span:
            for j, _ in links[i]:
                if key[j] + 1e-6 > key[i]:
                    key[i] = key[j] + 1e-6
        return sorted(range(n), key=lambda i: key[i])

    zero, tail = [0.0] * n, [d[1] - d[0] for d in dur]
    rest = [0.0] * n
    for i in range(n - 1, -1, -1):
        rest[i] = max([rest[k] + lag(i, k) for k, _ in back[i]] + [dur[i][1]])
    key, found, rnd = [-r for r in rest], [], 1
    base, low = key, 1e9
    for step in range(PASSES):
        start = fill(ranked(key, fore, range(n)), fore, zero)
        end = max(s + d[1] for s, d in zip(start, dur))
        found.append((end, start))
        late = fill(ranked([-s - d[0] for s, d in zip(start, dur)], back, range(n - 1, -1, -1)), back, tail)
        key = [-r - d[0] for r, d in zip(late, dur)]
        if end < low + SLACK:
            base, low = key, min(low, end)
        if step % 2 == 1:
            rnd = (rnd * 1103515245 + 12345) % (1 << 31)
            t0 = -low * ((rnd >> 8) % 1000) / 1000.0
            key = []
            for k in base:
                if t0 < k < t0 + SPAN:
                    rnd = (rnd * 1103515245 + 12345) % (1 << 31)
                    k += SHAKE * ((rnd >> 8) % 1000 - 500) / 500.0
                key.append(k)
    cur, start = min(found, key=lambda f: f[0])
    for step in range(MOVES):
        order = sorted(range(n), key=lambda i: (start[i], i))
        before, seen = {}, {}
        for i in order:
            before[i], seen[qs[i]] = seen.get(qs[i], -1), i
        i, pairs = max(range(n), key=lambda i: start[i] + dur[i][1]), []
        while start[i] > 1e-9:
            js = [j for j, w in fore[i] if start[j] + w > start[i] - 1e-7]
            if not js:
                pairs.append((before[i], i))
            i = js[0] if js else before[i]
        rnd = (rnd * 1103515245 + 12345) % (1 << 31)
        p, i = pairs[(rnd >> 8) % len(pairs)]
        key = list(start)
        far = 1e-4 + ((rnd >> 5) % 4) * 0.3
        if (rnd >> 4) & 1:
            key[p] = start[i] + far
        else:
            key[i] = start[p] - far
            for k in range(i, -1, -1):
                for j, _ in fore[k]:
                    if key[j] > key[k] - 1e-6:
                        key[j] = key[k] - 1e-6
        new = fill(ranked(key, fore, range(n)), fore, zero)
        if step % 4 == 0:
            late = fill(ranked([-s - d[0] for s, d in zip(new, dur)], back, range(n - 1, -1, -1)), back, tail)
            new = fill(ranked([-r - d[0] for r, d in zip(late, dur)], fore, range(n)), fore, zero)
        end = max(s + d[1] for s, d in zip(new, dur))
        if end <= cur + SLACK * (1.0 - step / MOVES) * ((rnd >> 12) % 100) / 100.0:
            cur, start = end, new
            found.append((end, new))
    found.sort(key=lambda f: f[0])
    return refine(ops, deps, [sorted(range(n), key=lambda i: (s[i], i)) for _, s in found[:TRIED]])


def refine(ops, deps, first):
    n = len(ops)
    cases = [([lasts(o, *c[:6]) for o in ops], c[6]) for c in CASES]
    qs = [o[0] for o in ops]
    kids = [[] for _ in ops]
    for i in range(n):
        for j in deps[i]:
            kids[j].append(i)

    def run(seq, case):
        dur, hop = cases[case]
        nxt, left, ready, why = [-1] * n, [len(d) for d in deps], [0.0] * n, [-1] * n
        for l in seq.values():
            for a, b in zip(l, l[1:]):
                nxt[a] = b
                left[b] += 1
        todo, order, end, tail = [i for i in range(n) if not left[i]], [], 0.0, -1
        while todo:
            i = todo.pop()
            order.append(i)
            hold, done = ready[i] + dur[i][0], ready[i] + dur[i][1]
            if done > end:
                end, tail = done, i
            for k in kids[i]:
                t = hold if qs[i] == qs[k] == "p" else done + hop
                if t > ready[k]:
                    ready[k], why[k] = t, i
                left[k] -= 1
                if not left[k]:
                    todo.append(k)
            k = nxt[i]
            if k >= 0:
                if hold > ready[k]:
                    ready[k], why[k] = hold, i
                left[k] -= 1
                if not left[k]:
                    todo.append(k)
        if len(order) < n:
            return 1e9, [], order, ready
        pairs = []
        while why[tail] >= 0:
            if nxt[why[tail]] == tail and why[tail] not in deps[tail]:
                pairs.append((why[tail], tail))
            tail = why[tail]
        return end, pairs, order, ready

    def score(seq):
        r = [run(seq, c) for c in range(len(cases))]
        return sum(x[0] / w for x, w in zip(r, WEIGHT)), [p for x in r for p in x[1]]

    seqs = [{q: [i for i in f if qs[i] == q] for q in sorted(set(qs))} for f in first]
    seq = min(seqs, key=lambda s: score(s)[0])
    cur, pairs = score(seq)
    best, keep, rnd = cur, {q: list(l) for q, l in seq.items()}, 12345
    for step in range(STEPS):
        rnd = (rnd * 1103515245 + 12345) % (1 << 31)
        a, b = pairs[(rnd >> 8) % len(pairs)]
        l = seq[qs[a]]
        k = l.index(a)
        old = list(l)
        far = (rnd >> 4) % 4
        if (rnd >> 3) & 1:
            l.insert(max(0, k - far), l.pop(k + 1))
        else:
            l.insert(k + 1 + far, l.pop(k))
        new, p2 = score(seq)
        if new <= cur + 0.004 * (1.0 - step / STEPS) * ((rnd >> 12) % 100) / 100.0:
            cur, pairs = new, p2
            if cur < best:
                best, keep = cur, {q: list(x) for q, x in seq.items()}
        else:
            seq[qs[a]] = old
    _, _, order, ready = run(keep, 0)
    place = {i: k for k, i in enumerate(order)}
    return sorted(range(n), key=lambda i: (ready[i], place[i]))


CASES = [(0.00083, 1.4, 3.3, 0.6, 2.2, 4.0, 0.12), (0.00112, 1.75, 4.5, 0.5, 2.0, 3.5, 0.12)]
WEIGHT = [75.0, 95.0]
STEPS, MOVES = 6000, 4000
PASSES, TRIED, SHAKE, SLACK, SPAN = 3000, 40, 1.0, 0.2, 4.0
HOP = 0.12
ORDER = []


def rank_program(g, core, T, topo):
    rank = T.rank_of(core)
    if rank is None:
        return
    ops = program(rank, T, topo)
    queue = {"v": g.vector, "a": g.scalar, "p": g.tensor, "g": g, "s": g.sync}

    def real(x):
        if not isinstance(x, tuple) or not x or x[0] not in ("ap", "ind", "raw"):
            return x
        if x[0] == "raw":
            return x[2]
        if x[0] == "ind":
            return real(x[1]).indirect(real(x[2]))
        _, name, c0, c1, step, p0, p1 = x
        return T[name][p0:p1, c0:c1:step] if step != 1 else T[name][p0:p1, c0:c1]

    touch, deps = [], []
    for q, call, args, kw, nout, extra in ops:
        wr, rd = [], []
        for x in list(args[:nout]) + list(extra):
            if x[0] == "ind":
                wr += spans(x[1]); rd += spans(x[2])
            else:
                wr += spans(x)
        for x in list(args[nout:]) + [v for k, v in kw.items() if k != "accum_out"]:
            rd += spans(x)
        dma = call in ("dma_start", "remote", "landed")
        mine = []
        for j, (q2, wr2, rd2, dma2) in enumerate(touch):
            hit = False
            for n, a, b in wr:
                for n2, a2, b2 in wr2 + rd2:
                    if n == n2 and a < b2 and a2 < b and not (dma and dma2 and (n2, a2, b2) not in rd2):
                        hit = True
            for n, a, b in rd:
                for n2, a2, b2 in wr2 + ([s for s in rd2 if s[0].endswith("_")] if q != q2 else []):
                    if n == n2 and a < b2 and a2 < b:
                        hit = True
            if call == "landed":
                hit = ops[j][1] == "remote" and ops[j][2][3] == args[1]
            if hit:
                mine.append(j)
        touch.append((q, wr, rd, dma))
        deps.append(mine)
    if not ORDER:
        gp = [i for i, o in enumerate(ops) if o[1] == "remote"]
        after = dict(zip(gp[1:], gp))
        ORDER.extend(arrange(ops, [d + ([after[i]] if i in after and after[i] not in d else []) for i, d in enumerate(deps)]))
    order = ORDER
    place = {i: k for k, i in enumerate(order)}
    deps = [sorted(place[j] for j in deps[i] if not ops[i][0] == ops[j][0] == "p") for i in order]
    ops, touch = [ops[i] for i in order], [touch[i] for i in order]
    need = []
    for i, mine in enumerate(deps):
        latest = {}
        keep = []
        for j in mine:
            if touch[j][3]:
                keep.append(j)
            else:
                latest[touch[j][0]] = j
        need.append(keep + list(latest.values()))
    wanted = set(j for m in need for j in m)
    mark, count, known, ndma, out = {}, {}, {k: {} for k in queue}, [0], [0]
    for i, (q, call, args, kw, nout, extra) in enumerate(ops):
        if call == "landed":
            mark[i] = (args[1], args[2])
            count[args[1]] = args[2]
            continue
        waits = {}
        for j in need[i]:
            if j in mark:
                s, n = mark[j]
                waits[s] = max(waits.get(s, 0), n)
        for s, n in waits.items():
            if known[q].get(s, 0) < n:
                queue[q].wait_ge(T.sem[s], n)
                known[q][s] = n
        if call == "remote":
            g.remote_dma_fused(args[1], local_sem=T.sem.out)
            out[0] += args[2]
            continue
        a, k = [real(x) for x in args], {n: real(x) for n, x in kw.items()}
        e = queue[q]
        if call == "dma_start" and len(args) > 2:
            s = args[2]
            e.dma_start(*a[:2]).then_inc(T.sem[s], 16)
            count[s] = 16 * sum(1 for o in ops if o[1] == call and o[2][2:] == [s])
            mark[i] = (s, count[s])
            continue
        if call == "dma_start":
            s = "d%d" % ndma[0]
            ndma[0] += 1
            e.dma_start(*a).then_inc(T.sem[s], 16)
            mark[i] = (s, 16)
            count[s] = 16
            continue
        ins = {"tensor_copy": lambda: e.tensor_copy(*a), "tensor_tensor": lambda: e.tensor_tensor(*a),
               "tensor_scalar": lambda: e.tensor_scalar(*a), "tensor_tensor_scan": lambda: e.tensor_tensor_scan(*a),
               "memset": lambda: e.memset(*a), "tensor_reduce": lambda: e.tensor_reduce(*a),
               "activation": lambda: e.activation(*a, **k), "matmul": lambda: e.matmul(*a),
               "iota": lambda: e.iota(*a, **k)}[call]()
        if i in wanted:
            s = "s" + q
            count[s] = count.get(s, 0) + 1
            ins.then_inc(T.sem[s], 1)
            mark[i] = (s, count[s])
    count["out"] = out[0]
    for s, n in count.items():
        if known["g"].get(s, 0) < n:
            g.wait_ge(T.sem[s], n)
